import numpy as np
import ml_dtypes


def mxq(x, axis, fmt="e4m3"):
    dtype, down = {"e4m3": (ml_dtypes.float8_e4m3fn, 7), "e5m2": (ml_dtypes.float8_e5m2, 14)}[fmt]
    v = np.moveaxis(np.asarray(x, np.float32).astype(ml_dtypes.bfloat16).astype(np.float64), axis, -1)
    blocks = v.reshape(v.shape[:-1] + (-1, 32))
    amax = np.abs(blocks).max(-1, keepdims=True)
    byte = np.maximum(np.where(amax > 0, np.frexp(amax)[1] - 1 + 127, 0) - down, 1)
    scale = np.exp2(byte - 127.0)
    codes = (blocks / scale).astype(np.float32).astype(dtype).astype(np.float64)
    return np.moveaxis((codes * scale).reshape(v.shape), -1, axis)


WIDE = False


def mx_kscale(k):
    if not WIDE:
        return np.ones(k)
    levels = np.array([10, -10, 5, -5, 0])
    if k % 512:
        return np.exp2(np.random.permutation(np.resize(levels, k // 32))).repeat(32)
    a = np.empty((k // 512, 16))
    for p in range(k // 512):
        a[p, :8] = np.random.permutation(np.resize(levels, 8))
        for g in range(8):
            far = levels[np.abs(levels - a[p, g]) >= 10]
            a[p, g + 8] = far[np.random.randint(len(far))]
    return np.exp2(a.ravel()).repeat(32)


def f64(x):
    return np.asarray(x).astype(np.float64)


def striped(idx):
    return np.tile(idx.reshape(-1, 16).T, (8, 1)).astype(np.uint16)


def unstriped(offs):
    return offs[:16].T.reshape(-1).astype(np.int64)


E2M1 = np.array([0.0, 0.5, 1.0, 1.5, 2.0, 3.0, 4.0, 6.0, -0.0, -0.5, -1.0, -1.5, -2.0, -3.0, -4.0, -6.0])


def pack_weight(w, fmt):
    k, n = w.shape
    w = f64(np.asarray(w, np.float32).astype(ml_dtypes.bfloat16)).reshape(k // 32, 32, n)
    amax = np.abs(w).max(1)
    if fmt == "e4m3":
        byte = np.frexp(amax)[1] - 1 + 127 - 7
    else:
        mant, ex = np.frexp(amax / 6.0)
        byte = np.where(mant > 0.5, ex, ex - 1) + 127
    byte = np.clip(np.where(amax > 0, byte, 1), 1, 254)
    scaled = (w * np.exp2(127.0 - byte)[:, None, :]).reshape(k, n).astype(np.float32)
    by_word = np.ascontiguousarray(scaled.reshape(k // 512, 128, 4, n).transpose(0, 1, 3, 2))
    if fmt == "e4m3":
        words = by_word.astype(ml_dtypes.float8_e4m3fn).view(np.uint8)
    else:
        c = by_word.astype(ml_dtypes.float4_e2m1fn).view(np.uint8) & 0xF
        words = (c[..., 0::2] | (c[..., 1::2] << 4)).reshape(k // 512, 128, 2 * n)
    return np.ascontiguousarray(words), np.ascontiguousarray(byte.astype(np.uint8).reshape(k // 512, 16, n))


def unpack_weight(words, scales, fmt):
    g, _, n = scales.shape
    words = np.ascontiguousarray(words).reshape(g, 128, n, -1)
    if fmt == "e4m3":
        vals = words.view(ml_dtypes.float8_e4m3fn).astype(np.float64)
    else:
        nib = np.empty((g, 128, n, 4), np.uint8)
        nib[..., 0::2] = words & 0xF
        nib[..., 1::2] = words >> 4
        vals = E2M1[nib]
    vals = vals * np.repeat(np.exp2(scales.astype(np.float64) - 127.0), 8, axis=1)[..., None]
    return vals.transpose(0, 1, 3, 2).reshape(g * 512, n)


def relu(v):
    return np.maximum(v, 0.0)


K, T, E, C, H, N = 1024, 768, 12, 256, 512, 128
TOP = 4


def by_expert(wq, xq):
    return np.concatenate([wq[e].T @ xq[:, e * C:(e + 1) * C] for e in range(E)], axis=1)


def setup_inputs():
    n = np.random.standard_normal
    s = mx_kscale(K)[:, None]
    u = mx_kscale(H)
    deal = np.repeat(np.arange(E), C).reshape(TOP, T)[:, np.random.permutation(T)]
    deal = np.take_along_axis(deal, np.argsort(np.random.rand(TOP, T), axis=0), axis=0)
    for _ in range(8):
        s_, t_ = np.random.permutation(T).reshape(2, -1); r = np.random.randint(TOP, size=T // 2); x, y = deal[r, s_].copy(), deal[r, t_].copy()
        ok = ~((deal[:, s_] == y).any(0) | (deal[:, t_] == x).any(0)); deal[r[ok], s_[ok]] = y[ok]; deal[r[ok], t_[ok]] = x[ok]
    order = np.lexsort((np.random.rand(TOP * T), deal.reshape(-1)))
    slot_token = order % T; pos = np.empty(TOP * T, np.int64); pos[order] = np.arange(TOP * T); pos = pos.reshape(TOP, T)
    g = np.random.uniform(0.5, 1.5, (TOP, T)); g = g / g.sum(0)
    w1 = [pack_weight(m, "e2m1") for m in n((E, K, H)) / np.sqrt(K) / s[None] * u[None, None, :]]
    w2 = [pack_weight(m, "e2m1") for m in n((E, H, N)) / np.sqrt(H) / u[None, :, None]]
    x = pack_weight(n((K, T)) * s, "e4m3")
    return {
        "x_words": x[0],
        "x_scales": x[1],
        "w1_words": np.stack([m[0] for m in w1]),
        "w1_scales": np.stack([m[1] for m in w1]),
        "w2_words": np.stack([m[0] for m in w2]),
        "w2_scales": np.stack([m[1] for m in w2]),
        "gate": np.stack([np.tile(r, (N, 1)) for r in g]).astype(np.float32),
        "offs": striped(slot_token),
        "pos1": striped(pos[0]),
        "pos2": striped(pos[1]),
        "pos3": striped(pos[2]),
        "pos4": striped(pos[3]),
    }


def reference(x_words, x_scales, w1_words, w1_scales, w2_words, w2_scales, gate, offs, pos1, pos2, pos3, pos4):
    idx = unstriped(offs)
    w1 = np.stack([unpack_weight(w1_words[e], w1_scales[e], "e2m1") for e in range(E)])
    w2 = np.stack([unpack_weight(w2_words[e], w2_scales[e], "e2m1") for e in range(E)])
    xq = unpack_weight(x_words, x_scales, "e4m3")[:, idx]
    h = relu(by_expert(w1, xq))
    y = by_expert(w2, mxq(h, 0, "e4m3"))
    return sum(f64(gate[r]) * y[:, unstriped(p)] for r, p in enumerate((pos1, pos2, pos3, pos4)))

@@ -1,0 +1,245 @@
+from contextlib import ExitStack
+
+import concourse.mybir as mybir
+from concourse.masks import make_identity
+
+K, T, E, C, H, N = 1024, 768, 12, 256, 512, 128
+TOP = 4
+S = E * C
+P = 128
+FLOPS = 2 * S * (K * H + H * N)
+
+F32 = mybir.dt.float32
+BF16 = mybir.dt.bfloat16
+I32 = mybir.dt.int32
+U32 = mybir.dt.uint32
+U16 = mybir.dt.uint16
+U8 = mybir.dt.uint8
+FP8X4 = mybir.dt.float8_e4m3fn_x4
+FP4X4 = mybir.dt.float4_e2m1fn_x4
+RELU = mybir.ActivationFunctionType.Relu
+MULT = mybir.AluOpType.mult
+ADD = mybir.AluOpType.add
+
+SCALE_CHUNKS = [(0, 1), (1, 2), (2, 3), (3, 4), (4, 6), (6, 8), (8, 10), (10, 12)]
+SCALE_BUFFER = [0, 1, 2, 3, 0, 1, 3, 0]
+G = 3
+OUT_CHUNKS = [(0, 320), (320, 640), (640, 768)]
+A_BANKS = 3
+T_BANKS = 5
+LAG = 4
+
+
+def tile_moe_pkd_mlp_relu_kernel(tc, x_words, x_scales, w1_words, w1_scales, w2_words, w2_scales, gate, offs, pos1, pos2, pos3, pos4, out):
+    nc = tc.nc
+    with ExitStack() as ctx:
+        lists = ctx.enter_context(tc.tile_pool(name="lists", bufs=1))
+        keep = ctx.enter_context(tc.tile_pool(name="keep", bufs=1))
+        wring = ctx.enter_context(tc.tile_pool(name="wring", bufs=3))
+        gring = ctx.enter_context(tc.tile_pool(name="gring", bufs=3))
+        hring = ctx.enter_context(tc.tile_pool(name="hring", bufs=6))
+        psum = ctx.enter_context(tc.psum_pool(name="psum", bufs=1))
+
+        offs_t = lists.tile([P, S // 16], U16, name="offs_t")
+        pos_t = [lists.tile([P, T // 16], U16, name="pos_t%d" % r) for r in range(TOP)]
+        a_bank = [psum.tile([P, H], F32, name="a_bank%d" % b) for b in range(A_BANKS)]
+        t_bank = [psum.tile([P, H], F32, name="t_bank%d" % b) for b in range(T_BANKS)]
+
+        xs = keep.tile([P, T], U8, name="xs", align_bytes=64)
+        xw = keep.tile([P, 2, T], U32, name="xw", align_bytes=64)
+        plane = keep.tile([P, 4 * G, H], U8, name="plane", align_bytes=64)
+        y_all = keep.tile([P, S], F32, name="y_all")
+        ident = keep.tile([P, P], F32, name="ident")
+        warm = keep.tile([P, 8], F32, name="warm")
+
+        gathered = keep.tile([P, 4, 2 * C], U8, name="gathered", align_bytes=64)
+        shifted = keep.tile([P, 4, 2 * C], U8, name="shifted", align_bytes=64)
+        w2w = keep.tile([P, E, 2 * N], U8, name="w2w", align_bytes=64)
+        nc.vector.memset(plane[:].bitcast(I32), 0)
+        nc.vector.memset(warm[:], 0.0)
+        nc.vector.memset(shifted[:].bitcast(I32), 0)
+
+        xs_i = xs[:].bitcast(I32)
+        xs_d = x_scales.bitcast(I32).rearrange("o f t -> (o f) t")
+        nc.sync.dma_start(offs_t[:], offs)
+        nc.scalar.dma_start(xs_i[0:112, :], xs_d[0:28, :].unsqueeze(0).broadcast_to([4, 28, T // 4]))
+        nc.sync.dma_start(xs_i[112:128, :], xs_d[28:32, :].unsqueeze(0).broadcast_to([4, 4, T // 4]))
+        nc.sync.dma_start(xw[:].bitcast(I32), x_words.rearrange("o p t r -> p o (t r)").bitcast(I32))
+
+        def load_w1_scales(a, b):
+            src = w1_scales[a:b].bitcast(I32).rearrange("e s q n -> q (e s) n")
+            place = 2 * (a % (2 * G))
+            for q in range(4):
+                nc.sync.dma_start(plane[32 * q : 32 * q + 4, place : place + 2 * (b - a), :].bitcast(I32), src[4 * q : 4 * q + 4, :, :])
+
+        w1w = {}
+
+        def load_w1_words(g, cuts):
+            slot = wring.tile([P, 2 * G, 2 * H], U8, name="slot", align_bytes=64)
+            for a, b in cuts:
+                src = w1_words[G * g + a : G * g + b].bitcast(I32).rearrange("e s p n -> p (e s) n")
+                nc.gpsimd.dma_start(slot[:, 2 * a : 2 * b, :].bitcast(I32), src)
+            w1w[g] = slot
+
+        w2s = plane[:].rearrange("p a n -> p (a n)")
+
+        def load_w2():
+            nc.gpsimd.dma_start(w2w[:].bitcast(I32), w2_words.bitcast(I32).rearrange("e s p n -> p (e s) n"))
+
+        def load_w2_scales():
+            src = w2_scales.bitcast(I32).rearrange("e s q n -> q (e s) n")
+            for q in range(4):
+                dst = w2s[32 * q : 32 * q + 4, 0 : E * N].bitcast(I32).rearrange("p (e n) -> p e n", e=E)
+                nc.sync.dma_start(dst, src[4 * q : 4 * q + 4, :, :])
+
+        gate_t = []
+
+        def load_gate(r):
+            slot = wring.tile([P, 2, T], F32, name="slot", align_bytes=64)
+            nc.gpsimd.dma_start(slot[:], gate[r : r + 2].rearrange("r p t -> p r t"))
+            gate_t.append(slot[:, 0, :])
+            gate_t.append(slot[:, 1, :])
+
+        gs = {}
+
+        def gather_scales(c):
+            a, b = SCALE_CHUNKS[c]
+            w = (b - a) * C
+            g0 = gathered[:, SCALE_BUFFER[c], 0:w]
+            g1 = shifted[:, SCALE_BUFFER[c], 0:w]
+            nc.vector.tensor_copy(g0, xs[:].indirect(offs_t[:, a * C // 16 : b * C // 16]))
+            nc.sync.dma_start(g1[0:112, :].bitcast(I32), g0[16:128, :].bitcast(I32))
+            for j in range(0, w, P):
+                gs[a * C + j] = (g0[:, j : j + P], g1[:, j : j + P])
+
+        gw = {}
+
+        def gather_words(e):
+            for o in range(2):
+                g = gring.tile([P, C], U32, name="gw%d" % o, align_bytes=64)
+                nc.vector.tensor_copy(g[:], xw[:, o, :].indirect(offs_t[:, e * C // 16 : (e + 1) * C // 16]))
+                gw[(e, o)] = g
+
+        h_rows = {}
+
+        def layer1(e, half):
+            acc = a_bank[(2 * e + half) % A_BANKS]
+            for o in range(2):
+                nc.tensor.matmul_mx(
+                    out=acc[:],
+                    lhsT=gw[(e, o)][:, half * P : (half + 1) * P].bitcast(FP8X4),
+                    lhsT_scale=gs[e * C + half * P][o],
+                    rhs=w1w[e // G][:, 2 * (e % G) + o, :].bitcast(FP4X4),
+                    rhs_scale=plane[:, 2 * (e % (2 * G)) + o, :],
+                    start=(o == 0),
+                    stop=(o == 1),
+                )
+            hr = hring.tile([P, H], BF16, name="hr")
+            dst = hr[:].rearrange("j (u p d) -> j u p d", u=2, d=2)
+            src = acc[:].rearrange("j (p u d) -> j u p d", u=2, d=2)
+            nc.scalar.activation(dst, src, RELU)
+            h_rows[(e, half)] = hr
+
+        h_cols = {}
+
+        def turn(e):
+            tp = t_bank[e % T_BANKS][:].rearrange("p (a u j) -> p a u j", a=2, u=2)
+            for half in range(2):
+                words = h_rows[(e, half)][:].bitcast(F32)
+                for u in range(2):
+                    nc.tensor.transpose(tp[:, half, u, :], words[:, u * P : (u + 1) * P], ident[:])
+            hc = keep.tile([P, 4 * C], BF16, name="hc%d" % e, align_bytes=64)
+            dst = hc[:].bitcast(F32).rearrange("p (a j u) -> p a j u", a=2, u=2)
+            nc.scalar.copy(dst, tp.rearrange("p a u j -> p a j u"))
+            h_cols[e] = hc
+
+        h_q = {}
+
+        def quantise(e):
+            hq = keep.tile([P, C], U32, name="hq%d" % e, align_bytes=64)
+            hs = keep.tile([P, C], U8, name="hs%d" % e, align_bytes=64)
+            nc.vector.quantize_mx(out=hq[:].bitcast(FP8X4), scales=hs[:], in_=h_cols[e][:])
+            h_q[e] = (hq, hs)
+
+        def layer2(e, bank):
+            hq, hs = h_q[e]
+            nc.tensor.matmul_mx(
+                out=bank,
+                lhsT=w2w[:, e, :].bitcast(FP4X4),
+                lhsT_scale=w2s[:, e * N : (e + 1) * N],
+                rhs=hq[:].bitcast(FP8X4),
+                rhs_scale=hs[:],
+                start=True,
+                stop=True,
+            )
+
+        load_w1_scales(0, 2 * G)
+        load_w1_words(0, [(0, 1), (1, 3)])
+        nc.scalar.activation(warm[:, 0:1], warm[:, 1:2], RELU)
+        make_identity(nc, ident[:])
+        for c in range(4):
+            gather_scales(c)
+        for e in range(3):
+            gather_words(e)
+        load_w1_words(1, [(0, 3)])
+        load_w1_words(2, [(0, 3)])
+        load_w2()
+        for e in range(E):
+            layer1(e, 0)
+            if e >= 1:
+                turn(e - 1)
+            layer1(e, 1)
+            if e == 0:
+                gather_scales(4)
+            if e + 3 < E:
+                gather_words(e + 3)
+            if e in (1, 3, 5):
+                gather_scales(5 + e // 2)
+            if e == 2:
+                load_w1_words(3, [(0, 3)])
+            if e == 5:
+                load_gate(0)
+            if e == 8:
+                load_gate(2)
+            if e in (2, 5):
+                load_w1_scales(e + 4, e + 4 + G)
+            if e == 8:
+                load_w2_scales()
+            if e == 3:
+                for r, pos in enumerate((pos1, pos2, pos3, pos4)):
+                    nc.sync.dma_start(pos_t[r][:], pos)
+            if e >= 2:
+                quantise(e - 2)
+        turn(E - 1)
+        quantise(E - 2)
+        quantise(E - 1)
+        y_banks = [t_bank[2], t_bank[3], t_bank[4], t_bank[0], t_bank[1]]
+        for pair in range(5):
+            for j in range(2):
+                layer2(2 * pair + j, y_banks[pair][:, j * C : (j + 1) * C])
+            dst = y_all[:, 2 * pair * C : (2 * pair + 2) * C]
+            if pair in (0, 1, 2):
+                nc.vector.tensor_copy(dst, y_banks[pair][:])
+            else:
+                nc.scalar.copy(dst, y_banks[pair][:])
+        layer2(E - 2, a_bank[1][:, 0:C])
+        nc.scalar.copy(y_all[:, (E - 2) * C : (E - 1) * C], a_bank[1][:, 0:C])
+        layer2(E - 1, a_bank[2][:, 0:C])
+        nc.vector.tensor_copy(y_all[:, (E - 1) * C : E * C], a_bank[2][:, 0:C])
+
+        for a, b in OUT_CHUNKS:
+            w = b - a
+            prod = keep.tile([P, TOP, w], F32, name="prod%d" % a)
+            sums = keep.tile([P, TOP - 1, w], F32, name="sums%d" % a)
+
+            def fetch(r):
+                nc.vector.tensor_tensor(prod[:, r, :], y_all[:].indirect(pos_t[r][:, a // 16 : b // 16]), gate_t[r][:, a:b], MULT)
+
+            fetch(0)
+            fetch(1)
+            fetch(2)
+            nc.vector.tensor_tensor(sums[:, 0, :], prod[:, 0, :], prod[:, 1, :], ADD)
+            fetch(3)
+            nc.vector.tensor_tensor(sums[:, 1, :], sums[:, 0, :], prod[:, 2, :], ADD)
+            nc.vector.tensor_tensor(sums[:, 2, :], sums[:, 1, :], prod[:, 3, :], ADD)
+            nc.sync.dma_start(out[:, a:b], sums[:, 2, :])

@@ -24,6 +24,7 @@ ADD = mybir.AluOpType.add
 SCALE_CHUNKS = [(0, 1), (1, 2), (2, 3), (3, 4), (4, 6), (6, 8), (8, 10), (10, 12)]
 SCALE_BUFFER = [0, 1, 2, 3, 0, 1, 3, 0]
 G = 3
+SLOTS = 8
 OUT_CHUNKS = [(0, 320), (320, 640), (640, 768)]
 A_BANKS = 3
 T_BANKS = 5
@@ -35,7 +36,6 @@ def tile_moe_pkd_mlp_relu_kernel(tc, x_words, x_scales, w1_words, w1_scales, w2_
     with ExitStack() as ctx:
         lists = ctx.enter_context(tc.tile_pool(name="lists", bufs=1))
         keep = ctx.enter_context(tc.tile_pool(name="keep", bufs=1))
-        wring = ctx.enter_context(tc.tile_pool(name="wring", bufs=3))
         gring = ctx.enter_context(tc.tile_pool(name="gring", bufs=3))
         hring = ctx.enter_context(tc.tile_pool(name="hring", bufs=6))
         psum = ctx.enter_context(tc.psum_pool(name="psum", bufs=1))
@@ -47,7 +47,7 @@ def tile_moe_pkd_mlp_relu_kernel(tc, x_words, x_scales, w1_words, w1_scales, w2_
 
         xs = keep.tile([P, T], U8, name="xs", align_bytes=64)
         xw = keep.tile([P, 2, T], U32, name="xw", align_bytes=64)
-        plane = keep.tile([P, 4 * G, H], U8, name="plane", align_bytes=64)
+        plane = keep.tile([P, 2 * SLOTS, H], U8, name="plane", align_bytes=64)
         y_all = keep.tile([P, S], F32, name="y_all")
         ident = keep.tile([P, P], F32, name="ident")
         warm = keep.tile([P, 8], F32, name="warm")
@@ -55,8 +55,10 @@ def tile_moe_pkd_mlp_relu_kernel(tc, x_words, x_scales, w1_words, w1_scales, w2_
         gathered = keep.tile([P, 4, 2 * C], U8, name="gathered", align_bytes=64)
         shifted = keep.tile([P, 4, 2 * C], U8, name="shifted", align_bytes=64)
         w2w = keep.tile([P, E, 2 * N], U8, name="w2w", align_bytes=64)
-        nc.vector.memset(plane[:].bitcast(I32), 0)
+        nc.vector.memset(plane[:, 0:4, :].bitcast(I32), 0)
         nc.vector.memset(warm[:], 0.0)
+        nc.vector.memset(ident[:], 0.0)
+        nc.vector.memset(plane[:, 4:, :].bitcast(I32), 0)
         nc.vector.memset(shifted[:].bitcast(I32), 0)
 
         xs_i = xs[:].bitcast(I32)
@@ -64,24 +66,23 @@ def tile_moe_pkd_mlp_relu_kernel(tc, x_words, x_scales, w1_words, w1_scales, w2_
         nc.sync.dma_start(offs_t[:], offs)
         nc.scalar.dma_start(xs_i[0:112, :], xs_d[0:28, :].unsqueeze(0).broadcast_to([4, 28, T // 4]))
         nc.sync.dma_start(xs_i[112:128, :], xs_d[28:32, :].unsqueeze(0).broadcast_to([4, 4, T // 4]))
-        nc.sync.dma_start(xw[:].bitcast(I32), x_words.rearrange("o p t r -> p o (t r)").bitcast(I32))
+        nc.gpsimd.dma_start(xw[:].bitcast(I32), x_words.rearrange("o p t r -> p o (t r)").bitcast(I32))
 
-        def load_w1_scales(a, b):
+        def load_w1_scales(a, b, queue):
             src = w1_scales[a:b].bitcast(I32).rearrange("e s q n -> q (e s) n")
-            place = 2 * (a % (2 * G))
+            place = 2 * (a % SLOTS)
             for q in range(4):
-                nc.sync.dma_start(plane[32 * q : 32 * q + 4, place : place + 2 * (b - a), :].bitcast(I32), src[4 * q : 4 * q + 4, :, :])
+                queue.dma_start(plane[32 * q : 32 * q + 4, place : place + 2 * (b - a), :].bitcast(I32), src[4 * q : 4 * q + 4, :, :])
 
         w1w = {}
 
-        def load_w1_words(g, cuts):
-            slot = wring.tile([P, 2 * G, 2 * H], U8, name="slot", align_bytes=64)
-            for a, b in cuts:
-                src = w1_words[G * g + a : G * g + b].bitcast(I32).rearrange("e s p n -> p (e s) n")
-                nc.gpsimd.dma_start(slot[:, 2 * a : 2 * b, :].bitcast(I32), src)
-            w1w[g] = slot
+        def load_w1_words(a, b):
+            words = keep.tile([P, 2 * (b - a), 2 * H], U8, name="w1w%d" % a, align_bytes=64)
+            nc.gpsimd.dma_start(words[:].bitcast(I32), w1_words[a:b].bitcast(I32).rearrange("e s p n -> p (e s) n"))
+            for e in range(a, b):
+                w1w[e] = words[:, 2 * (e - a) : 2 * (e - a) + 2, :]
 
-        w2s = plane[:].rearrange("p a n -> p (a n)")
+        w2s = plane[:, 8:12, :].rearrange("p a n -> p (a n)")
 
         def load_w2():
             nc.gpsimd.dma_start(w2w[:].bitcast(I32), w2_words.bitcast(I32).rearrange("e s p n -> p (e s) n"))
@@ -92,13 +93,7 @@ def tile_moe_pkd_mlp_relu_kernel(tc, x_words, x_scales, w1_words, w1_scales, w2_
                 dst = w2s[32 * q : 32 * q + 4, 0 : E * N].bitcast(I32).rearrange("p (e n) -> p e n", e=E)
                 nc.sync.dma_start(dst, src[4 * q : 4 * q + 4, :, :])
 
-        gate_t = []
-
-        def load_gate(r):
-            slot = wring.tile([P, 2, T], F32, name="slot", align_bytes=64)
-            nc.gpsimd.dma_start(slot[:], gate[r : r + 2].rearrange("r p t -> p r t"))
-            gate_t.append(slot[:, 0, :])
-            gate_t.append(slot[:, 1, :])
+        gate_t = keep.tile([P, TOP, T], F32, name="gate_t")
 
         gs = {}
 
@@ -116,9 +111,12 @@ def tile_moe_pkd_mlp_relu_kernel(tc, x_words, x_scales, w1_words, w1_scales, w2_
 
         def gather_words(e):
             for o in range(2):
-                g = gring.tile([P, C], U32, name="gw%d" % o, align_bytes=64)
-                nc.vector.tensor_copy(g[:], xw[:, o, :].indirect(offs_t[:, e * C // 16 : (e + 1) * C // 16]))
-                gw[(e, o)] = g
+                gw[(e, o)] = gring.tile([P, C], U32, name="gw%d" % o, align_bytes=64)
+            step = P if e == E - 1 else C
+            for j in range(0, C, step):
+                for o in range(2):
+                    first = e * C + j
+                    nc.vector.tensor_copy(gw[(e, o)][:, j : j + step], xw[:, o, :].indirect(offs_t[:, first // 16 : (first + step) // 16]))
 
         h_rows = {}
 
@@ -129,8 +127,8 @@ def tile_moe_pkd_mlp_relu_kernel(tc, x_words, x_scales, w1_words, w1_scales, w2_
                     out=acc[:],
                     lhsT=gw[(e, o)][:, half * P : (half + 1) * P].bitcast(FP8X4),
                     lhsT_scale=gs[e * C + half * P][o],
-                    rhs=w1w[e // G][:, 2 * (e % G) + o, :].bitcast(FP4X4),
-                    rhs_scale=plane[:, 2 * (e % (2 * G)) + o, :],
+                    rhs=w1w[e][:, o, :].bitcast(FP4X4),
+                    rhs_scale=plane[:, 2 * (e % SLOTS) + o, :],
                     start=(o == 0),
                     stop=(o == 1),
                 )
@@ -140,92 +138,101 @@ def tile_moe_pkd_mlp_relu_kernel(tc, x_words, x_scales, w1_words, w1_scales, w2_
             nc.scalar.activation(dst, src, RELU)
             h_rows[(e, half)] = hr
 
-        h_cols = {}
+        h_cols = keep.tile([P, 4 * S], BF16, name="h_cols", align_bytes=64)
 
-        def turn(e):
-            tp = t_bank[e % T_BANKS][:].rearrange("p (a u j) -> p a u j", a=2, u=2)
-            for half in range(2):
+        def turn(e, halves, bank):
+            n = len(halves)
+            tp = bank[:, 0 : n * 2 * P].rearrange("p (a u j) -> p a u j", a=n, u=2)
+            for a, half in enumerate(halves):
                 words = h_rows[(e, half)][:].bitcast(F32)
                 for u in range(2):
-                    nc.tensor.transpose(tp[:, half, u, :], words[:, u * P : (u + 1) * P], ident[:])
-            hc = keep.tile([P, 4 * C], BF16, name="hc%d" % e, align_bytes=64)
-            dst = hc[:].bitcast(F32).rearrange("p (a j u) -> p a j u", a=2, u=2)
+                    nc.tensor.transpose(tp[:, a, u, :], words[:, u * P : (u + 1) * P], ident[:])
+            first = e * C + halves[0] * P
+            dst = h_cols[:, 4 * first : 4 * (first + n * P)].bitcast(F32).rearrange("p (a j u) -> p a j u", a=n, u=2)
             nc.scalar.copy(dst, tp.rearrange("p a u j -> p a j u"))
-            h_cols[e] = hc
 
-        h_q = {}
+        EARLY = 6 * C
+        h_scales = keep.tile([P, S], U8, name="h_scales", align_bytes=64)
+        h_late = keep.tile([P, S - EARLY], U32, name="h_late", align_bytes=64)
+        h_early = []
 
-        def quantise(e):
-            hq = keep.tile([P, C], U32, name="hq%d" % e, align_bytes=64)
-            hs = keep.tile([P, C], U8, name="hs%d" % e, align_bytes=64)
-            nc.vector.quantize_mx(out=hq[:].bitcast(FP8X4), scales=hs[:], in_=h_cols[e][:])
-            h_q[e] = (hq, hs)
+        def h_words(a, b):
+            return h_early[0][:, a:b] if a < EARLY else h_late[:, a - EARLY : b - EARLY]
 
-        def layer2(e, bank):
-            hq, hs = h_q[e]
-            nc.tensor.matmul_mx(
-                out=bank,
-                lhsT=w2w[:, e, :].bitcast(FP4X4),
-                lhsT_scale=w2s[:, e * N : (e + 1) * N],
-                rhs=hq[:].bitcast(FP8X4),
-                rhs_scale=hs[:],
-                start=True,
-                stop=True,
-            )
+        def quantise(a, b):
+            nc.vector.quantize_mx(out=h_words(a, b).bitcast(FP8X4), scales=h_scales[:, a:b], in_=h_cols[:, 4 * a : 4 * b])
 
-        load_w1_scales(0, 2 * G)
-        load_w1_words(0, [(0, 1), (1, 3)])
+        def layer2(a, b, bank):
+            step = min(C, b - a)
+            for j in range(a, b, step):
+                e = j // C
+                nc.tensor.matmul_mx(
+                    out=bank[:, j - a : j - a + step],
+                    lhsT=w2w[:, e, :].bitcast(FP4X4),
+                    lhsT_scale=w2s[:, e * N : (e + 1) * N],
+                    rhs=h_words(j, j + step).bitcast(FP8X4),
+                    rhs_scale=h_scales[:, j : j + step],
+                    start=True,
+                    stop=True,
+                )
+
+        load_w1_scales(0, 2, nc.sync)
+        load_w1_words(0, 3)
         nc.scalar.activation(warm[:, 0:1], warm[:, 1:2], RELU)
-        make_identity(nc, ident[:])
+        make_identity(nc, ident[:], nomemset=True)
         for c in range(4):
             gather_scales(c)
         for e in range(3):
             gather_words(e)
-        load_w1_words(1, [(0, 3)])
-        load_w1_words(2, [(0, 3)])
+        load_w1_scales(2, SLOTS, nc.gpsimd)
+        load_w1_words(3, 6)
+        load_w1_words(6, 9)
+        load_w1_words(9, E)
         load_w2()
+        nc.gpsimd.dma_start(gate_t[:], gate.rearrange("r p t -> p r t"))
         for e in range(E):
             layer1(e, 0)
-            if e >= 1:
-                turn(e - 1)
             layer1(e, 1)
+            if e >= 1:
+                turn(e - 1, (0, 1), t_bank[(e - 1) % T_BANKS])
             if e == 0:
                 gather_scales(4)
             if e + 3 < E:
                 gather_words(e + 3)
             if e in (1, 3, 5):
                 gather_scales(5 + e // 2)
-            if e == 2:
-                load_w1_words(3, [(0, 3)])
+            if e == 3:
+                load_w1_scales(SLOTS, E, nc.sync)
             if e == 5:
-                load_gate(0)
-            if e == 8:
-                load_gate(2)
-            if e in (2, 5):
-                load_w1_scales(e + 4, e + 4 + G)
-            if e == 8:
                 load_w2_scales()
             if e == 3:
                 for r, pos in enumerate((pos1, pos2, pos3, pos4)):
                     nc.sync.dma_start(pos_t[r][:], pos)
-            if e >= 2:
-                quantise(e - 2)
-        turn(E - 1)
-        quantise(E - 2)
-        quantise(E - 1)
-        y_banks = [t_bank[2], t_bank[3], t_bank[4], t_bank[0], t_bank[1]]
-        for pair in range(5):
-            for j in range(2):
-                layer2(2 * pair + j, y_banks[pair][:, j * C : (j + 1) * C])
-            dst = y_all[:, 2 * pair * C : (2 * pair + 2) * C]
-            if pair in (0, 1, 2):
-                nc.vector.tensor_copy(dst, y_banks[pair][:])
+        last = E - 1
+        turn(last, (0,), t_bank[1])
+        turn(last, (1,), t_bank[2])
+        h_early.append(keep.tile([P, EARLY], U32, name="w1w6", align_bytes=64))
+        for a in range(0, (E - 2) * C, 2 * C):
+            quantise(a, a + 2 * C)
+        pieces = [
+            (0, 2 * C, a_bank[0], True),
+            (2 * C, 4 * C, t_bank[4], True),
+            (4 * C, 6 * C, a_bank[1], False),
+            (6 * C, 8 * C, a_bank[2], False),
+            (8 * C, 10 * C, t_bank[0], False),
+            (10 * C, 11 * C, t_bank[3], False),
+            (11 * C, 11 * C + P, t_bank[1], True),
+            (11 * C + P, S, t_bank[2], True),
+        ]
+        for a, b, bank, on_vector in pieces:
+            if a >= (E - 2) * C:
+                quantise(a, b)
+        for a, b, bank, on_vector in pieces:
+            layer2(a, b, bank)
+            if on_vector:
+                nc.vector.tensor_copy(y_all[:, a:b], bank[:, 0 : b - a])
             else:
-                nc.scalar.copy(dst, y_banks[pair][:])
-        layer2(E - 2, a_bank[1][:, 0:C])
-        nc.scalar.copy(y_all[:, (E - 2) * C : (E - 1) * C], a_bank[1][:, 0:C])
-        layer2(E - 1, a_bank[2][:, 0:C])
-        nc.vector.tensor_copy(y_all[:, (E - 1) * C : E * C], a_bank[2][:, 0:C])
+                nc.scalar.copy(y_all[:, a:b], bank[:, 0 : b - a])
 
         for a, b in OUT_CHUNKS:
             w = b - a
@@ -233,7 +240,7 @@ def tile_moe_pkd_mlp_relu_kernel(tc, x_words, x_scales, w1_words, w1_scales, w2_
             sums = keep.tile([P, TOP - 1, w], F32, name="sums%d" % a)
 
             def fetch(r):
-                nc.vector.tensor_tensor(prod[:, r, :], y_all[:].indirect(pos_t[r][:, a // 16 : b // 16]), gate_t[r][:, a:b], MULT)
+                nc.vector.tensor_tensor(prod[:, r, :], y_all[:].indirect(pos_t[r][:, a // 16 : b // 16]), gate_t[:, r, a:b], MULT)
 
             fetch(0)
             fetch(1)

@@ -18,6 +18,7 @@ U8 = mybir.dt.uint8
 FP8X4 = mybir.dt.float8_e4m3fn_x4
 FP4X4 = mybir.dt.float4_e2m1fn_x4
 RELU = mybir.ActivationFunctionType.Relu
+COPY = mybir.ActivationFunctionType.Copy
 MULT = mybir.AluOpType.mult
 ADD = mybir.AluOpType.add
 
@@ -29,6 +30,8 @@ OUT_CHUNKS = [(0, 320), (320, 640), (640, 768)]
 A_BANKS = 3
 T_BANKS = 5
 LAG = 4
+BLOCKS = T // P
+HALF = T // 2
 
 
 def tile_moe_pkd_mlp_relu_kernel(tc, x_words, x_scales, w1_words, w1_scales, w2_words, w2_scales, gate, offs, pos1, pos2, pos3, pos4, out):
@@ -93,7 +96,10 @@ def tile_moe_pkd_mlp_relu_kernel(tc, x_words, x_scales, w1_words, w1_scales, w2_
                 dst = w2s[32 * q : 32 * q + 4, 0 : E * N].bitcast(I32).rearrange("p (e n) -> p e n", e=E)
                 nc.sync.dma_start(dst, src[4 * q : 4 * q + 4, :, :])
 
-        gate_t = keep.tile([P, TOP, T], F32, name="gate_t")
+        gate_last = keep.tile([P, T], F32, name="gate_last")
+        gate_rows = keep.tile([P, P], F32, name="gate_rows")
+        gate_cols = keep.tile([P, P], F32, name="gate_cols")
+        nc.vector.memset(gate_rows[:], 0.0)
 
         gs = {}
 
@@ -189,7 +195,8 @@ def tile_moe_pkd_mlp_relu_kernel(tc, x_words, x_scales, w1_words, w1_scales, w2_
         load_w1_words(6, 9)
         load_w1_words(9, E)
         load_w2()
-        nc.gpsimd.dma_start(gate_t[:], gate.rearrange("r p t -> p r t"))
+        nc.gpsimd.dma_start(gate_last[:], gate[TOP - 1])
+        nc.gpsimd.dma_start(gate_rows[0 : (TOP - 1) * BLOCKS, :], gate[0 : TOP - 1, 0, :].rearrange("r (c m) -> r c m", m=P))
         for e in range(E):
             layer1(e, 0)
             layer1(e, 1)
@@ -234,19 +241,53 @@ def tile_moe_pkd_mlp_relu_kernel(tc, x_words, x_scales, w1_words, w1_scales, w2_
             else:
                 nc.scalar.copy(y_all[:, a:b], bank[:, 0 : b - a])
 
-        for a, b in OUT_CHUNKS:
-            w = b - a
-            prod = keep.tile([P, TOP, w], F32, name="prod%d" % a)
-            sums = keep.tile([P, TOP - 1, w], F32, name="sums%d" % a)
+        nc.tensor.transpose(a_bank[0][:, 0:P], gate_rows[:], ident[:])
+        nc.scalar.copy(gate_cols[:, 0 : (TOP - 1) * BLOCKS], a_bank[0][:, 0 : (TOP - 1) * BLOCKS])
 
-            def fetch(r):
-                nc.vector.tensor_tensor(prod[:, r, :], y_all[:].indirect(pos_t[r][:, a // 16 : b // 16]), gate_t[:, r, a:b], MULT)
+        picked = keep.tile([P, TOP - 1, T], F32, name="picked")
+        scaled = keep.tile([P, TOP - 1, T], F32, name="scaled")
+        prod = keep.tile([P, T], F32, name="prod")
+        total = keep.tile([P, T], F32, name="total")
+        fwd_banks = [t_bank[4], a_bank[1], a_bank[2], a_bank[0]]
+        sum_banks = [t_bank[0], t_bank[3], t_bank[1], t_bank[2]]
+        per_half = HALF // P
 
-            fetch(0)
-            fetch(1)
-            fetch(2)
-            nc.vector.tensor_tensor(sums[:, 0, :], prod[:, 0, :], prod[:, 1, :], ADD)
-            fetch(3)
-            nc.vector.tensor_tensor(sums[:, 1, :], sums[:, 0, :], prod[:, 2, :], ADD)
-            nc.vector.tensor_tensor(sums[:, 2, :], sums[:, 1, :], prod[:, 3, :], ADD)
-            nc.sync.dma_start(out[:, a:b], sums[:, 2, :])
+        def sum_place(c):
+            if c < per_half:
+                return sum_banks[0][:, c * P : (c + 1) * P]
+            return sum_banks[1 + c - per_half][:, 0:P]
+
+        def back(r, c):
+            nc.tensor.matmul(sum_place(c), lhsT=scaled[:, r, c * P : (c + 1) * P], rhs=ident[:], is_transpose=True, start=(r == 0), stop=(r == TOP - 2))
+
+        for hf in range(2):
+            a = hf * HALF
+            for r in range(TOP - 1):
+                nc.vector.tensor_copy(picked[:, r, a : a + HALF], y_all[:].indirect(pos_t[r][:, a // 16 : (a + HALF) // 16]))
+                bank = fwd_banks[(hf * (TOP - 1) + r) % len(fwd_banks)]
+                blocks = range(hf * per_half, (hf + 1) * per_half)
+                for j, c in enumerate(blocks):
+                    nc.tensor.transpose(bank[:, j * P : (j + 1) * P], picked[:, r, c * P : (c + 1) * P], ident[:])
+                for j, c in enumerate(blocks):
+                    nc.scalar.activation(scaled[:, r, c * P : (c + 1) * P], bank[:, j * P : (j + 1) * P], COPY, scale=gate_cols[:, r * BLOCKS + c : r * BLOCKS + c + 1])
+                if hf == 1:
+                    for c in blocks:
+                        back(r, c)
+            if hf == 0:
+                for c in range(per_half):
+                    for r in range(TOP - 1):
+                        back(r, c)
+
+        def last_choice(a, b):
+            nc.vector.tensor_tensor(prod[:, a:b], y_all[:].indirect(pos_t[TOP - 1][:, a // 16 : b // 16]), gate_last[:, a:b], MULT)
+
+        last_choice(0, HALF)
+        last_choice(HALF, HALF + 2 * P)
+        nc.vector.tensor_tensor(total[:, 0:HALF], prod[:, 0:HALF], sum_banks[0][:, 0:HALF], ADD)
+        nc.sync.dma_start(out[:, 0:HALF], total[:, 0:HALF])
+        last_choice(HALF + 2 * P, T)
+        for c in range(per_half, BLOCKS):
+            nc.vector.tensor_tensor(total[:, c * P : (c + 1) * P], prod[:, c * P : (c + 1) * P], sum_place(c), ADD)
+            if c == BLOCKS - 2:
+                nc.sync.dma_start(out[:, HALF : HALF + 2 * P], total[:, HALF : HALF + 2 * P])
+        nc.sync.dma_start(out[:, T - P : T], total[:, T - P : T])

@@ -22,14 +22,15 @@ COPY = mybir.ActivationFunctionType.Copy
 MULT = mybir.AluOpType.mult
 ADD = mybir.AluOpType.add
 
-SCALE_CHUNKS = [(0, 1), (1, 2), (2, 3), (3, 4), (4, 6), (6, 8), (8, 10), (10, 12)]
-SCALE_BUFFER = [0, 1, 2, 3, 0, 1, 3, 0]
-G = 3
-SLOTS = 8
-OUT_CHUNKS = [(0, 320), (320, 640), (640, 768)]
+AHEAD = 3
+SCALE_BUFFERS = 4
+REFILL_AFTER = (0, 1, 3, 5)
+PLANE_EXPERTS = 8
+FIRST_PLANES = 2
+WEIGHT_RUN = 3
 A_BANKS = 3
 T_BANKS = 5
-LAG = 4
+EARLY = 6 * C
 BLOCKS = T // P
 HALF = T // 2
 
@@ -39,8 +40,8 @@ def tile_moe_pkd_mlp_relu_kernel(tc, x_words, x_scales, w1_words, w1_scales, w2_
     with ExitStack() as ctx:
         lists = ctx.enter_context(tc.tile_pool(name="lists", bufs=1))
         keep = ctx.enter_context(tc.tile_pool(name="keep", bufs=1))
-        gring = ctx.enter_context(tc.tile_pool(name="gring", bufs=3))
-        hring = ctx.enter_context(tc.tile_pool(name="hring", bufs=6))
+        gring = ctx.enter_context(tc.tile_pool(name="gring", bufs=AHEAD))
+        hring = ctx.enter_context(tc.tile_pool(name="hring", bufs=2 * AHEAD))
         psum = ctx.enter_context(tc.psum_pool(name="psum", bufs=1))
 
         offs_t = lists.tile([P, S // 16], U16, name="offs_t")
@@ -50,18 +51,17 @@ def tile_moe_pkd_mlp_relu_kernel(tc, x_words, x_scales, w1_words, w1_scales, w2_
 
         xs = keep.tile([P, T], U8, name="xs", align_bytes=64)
         xw = keep.tile([P, 2, T], U32, name="xw", align_bytes=64)
-        plane = keep.tile([P, 2 * SLOTS, H], U8, name="plane", align_bytes=64)
+        plane = keep.tile([P, 2 * PLANE_EXPERTS, H], U8, name="plane", align_bytes=64)
         y_all = keep.tile([P, S], F32, name="y_all")
         ident = keep.tile([P, P], F32, name="ident")
-        warm = keep.tile([P, 8], F32, name="warm")
+        zeros = keep.tile([P, P], F32, name="zeros")
 
-        gathered = keep.tile([P, 4, 2 * C], U8, name="gathered", align_bytes=64)
-        shifted = keep.tile([P, 4, 2 * C], U8, name="shifted", align_bytes=64)
+        gathered = keep.tile([P, SCALE_BUFFERS, 2 * C], U8, name="gathered", align_bytes=64)
+        shifted = keep.tile([P, SCALE_BUFFERS, 2 * C], U8, name="shifted", align_bytes=64)
         w2w = keep.tile([P, E, 2 * N], U8, name="w2w", align_bytes=64)
-        nc.vector.memset(plane[:, 0:4, :].bitcast(I32), 0)
-        nc.vector.memset(warm[:], 0.0)
-        nc.vector.memset(ident[:], 0.0)
-        nc.vector.memset(plane[:, 4:, :].bitcast(I32), 0)
+        nc.vector.memset(plane[:, 0 : 2 * FIRST_PLANES, :].bitcast(I32), 0)
+        nc.vector.memset(zeros[:], 0.0)
+        nc.vector.memset(plane[:, 2 * FIRST_PLANES :, :].bitcast(I32), 0)
         nc.vector.memset(shifted[:].bitcast(I32), 0)
 
         xs_i = xs[:].bitcast(I32)
@@ -73,22 +73,20 @@ def tile_moe_pkd_mlp_relu_kernel(tc, x_words, x_scales, w1_words, w1_scales, w2_
 
         def load_w1_scales(a, b, queue):
             src = w1_scales[a:b].bitcast(I32).rearrange("e s q n -> q (e s) n")
-            place = 2 * (a % SLOTS)
+            place = 2 * (a % PLANE_EXPERTS)
             for q in range(4):
                 queue.dma_start(plane[32 * q : 32 * q + 4, place : place + 2 * (b - a), :].bitcast(I32), src[4 * q : 4 * q + 4, :, :])
 
         w1w = {}
 
-        def load_w1_words(a, b):
-            words = keep.tile([P, 2 * (b - a), 2 * H], U8, name="w1w%d" % a, align_bytes=64)
+        def load_w1_words(a):
+            b = a + WEIGHT_RUN
+            words = keep.tile([P, 2 * WEIGHT_RUN, 2 * H], U8, name="w1w%d" % a, align_bytes=64)
             nc.gpsimd.dma_start(words[:].bitcast(I32), w1_words[a:b].bitcast(I32).rearrange("e s p n -> p (e s) n"))
             for e in range(a, b):
                 w1w[e] = words[:, 2 * (e - a) : 2 * (e - a) + 2, :]
 
         w2s = plane[:, 8:12, :].rearrange("p a n -> p (a n)")
-
-        def load_w2():
-            nc.gpsimd.dma_start(w2w[:].bitcast(I32), w2_words.bitcast(I32).rearrange("e s p n -> p (e s) n"))
 
         def load_w2_scales():
             src = w2_scales.bitcast(I32).rearrange("e s q n -> q (e s) n")
@@ -101,28 +99,30 @@ def tile_moe_pkd_mlp_relu_kernel(tc, x_words, x_scales, w1_words, w1_scales, w2_
         gate_cols = keep.tile([P, P], F32, name="gate_cols")
         nc.vector.memset(gate_rows[:], 0.0)
 
-        gs = {}
+        slot_scales = {}
+        buffer_of = {}
 
-        def gather_scales(c):
-            a, b = SCALE_CHUNKS[c]
-            w = (b - a) * C
-            g0 = gathered[:, SCALE_BUFFER[c], 0:w]
-            g1 = shifted[:, SCALE_BUFFER[c], 0:w]
-            nc.vector.tensor_copy(g0, xs[:].indirect(offs_t[:, a * C // 16 : b * C // 16]))
-            nc.sync.dma_start(g1[0:112, :].bitcast(I32), g0[16:128, :].bitcast(I32))
-            for j in range(0, w, P):
-                gs[a * C + j] = (g0[:, j : j + P], g1[:, j : j + P])
+        def gather_scales(a, b, buffer):
+            width = (b - a) * C
+            pass0 = gathered[:, buffer, 0:width]
+            pass1 = shifted[:, buffer, 0:width]
+            nc.vector.tensor_copy(pass0, xs[:].indirect(offs_t[:, a * C // 16 : b * C // 16]))
+            nc.sync.dma_start(pass1[0:112, :].bitcast(I32), pass0[16:128, :].bitcast(I32))
+            for j in range(0, width, P):
+                slot_scales[a * C + j] = (pass0[:, j : j + P], pass1[:, j : j + P])
+            for e in range(a, b):
+                buffer_of[e] = buffer
 
-        gw = {}
+        slot_words = {}
 
         def gather_words(e):
             for o in range(2):
-                gw[(e, o)] = gring.tile([P, C], U32, name="gw%d" % o, align_bytes=64)
+                slot_words[(e, o)] = gring.tile([P, C], U32, name="gw%d" % o, align_bytes=64)
             step = P if e == E - 1 else C
             for j in range(0, C, step):
                 for o in range(2):
                     first = e * C + j
-                    nc.vector.tensor_copy(gw[(e, o)][:, j : j + step], xw[:, o, :].indirect(offs_t[:, first // 16 : (first + step) // 16]))
+                    nc.vector.tensor_copy(slot_words[(e, o)][:, j : j + step], xw[:, o, :].indirect(offs_t[:, first // 16 : (first + step) // 16]))
 
         h_rows = {}
 
@@ -131,10 +131,10 @@ def tile_moe_pkd_mlp_relu_kernel(tc, x_words, x_scales, w1_words, w1_scales, w2_
             for o in range(2):
                 nc.tensor.matmul_mx(
                     out=acc[:],
-                    lhsT=gw[(e, o)][:, half * P : (half + 1) * P].bitcast(FP8X4),
-                    lhsT_scale=gs[e * C + half * P][o],
+                    lhsT=slot_words[(e, o)][:, half * P : (half + 1) * P].bitcast(FP8X4),
+                    lhsT_scale=slot_scales[e * C + half * P][o],
                     rhs=w1w[e][:, o, :].bitcast(FP4X4),
-                    rhs_scale=plane[:, 2 * (e % SLOTS) + o, :],
+                    rhs_scale=plane[:, 2 * (e % PLANE_EXPERTS) + o, :],
                     start=(o == 0),
                     stop=(o == 1),
                 )
@@ -147,26 +147,62 @@ def tile_moe_pkd_mlp_relu_kernel(tc, x_words, x_scales, w1_words, w1_scales, w2_
         h_cols = keep.tile([P, 4 * S], BF16, name="h_cols", align_bytes=64)
 
         def turn(e, halves, bank):
-            n = len(halves)
-            tp = bank[:, 0 : n * 2 * P].rearrange("p (a u j) -> p a u j", a=n, u=2)
+            count = len(halves)
+            turned = bank[:, 0 : count * 2 * P].rearrange("p (a u j) -> p a u j", a=count, u=2)
             for a, half in enumerate(halves):
-                words = h_rows[(e, half)][:].bitcast(F32)
+                pairs = h_rows[(e, half)][:].bitcast(F32)
                 for u in range(2):
-                    nc.tensor.transpose(tp[:, a, u, :], words[:, u * P : (u + 1) * P], ident[:])
+                    nc.tensor.transpose(turned[:, a, u, :], pairs[:, u * P : (u + 1) * P], ident[:])
             first = e * C + halves[0] * P
-            dst = h_cols[:, 4 * first : 4 * (first + n * P)].bitcast(F32).rearrange("p (a j u) -> p a j u", a=n, u=2)
-            nc.scalar.copy(dst, tp.rearrange("p a u j -> p a j u"))
+            dst = h_cols[:, 4 * first : 4 * (first + count * P)].bitcast(F32).rearrange("p (a j u) -> p a j u", a=count, u=2)
+            nc.scalar.copy(dst, turned.rearrange("p a u j -> p a j u"))
 
-        EARLY = 6 * C
+        load_w1_scales(0, FIRST_PLANES, nc.sync)
+        load_w1_words(0)
+        nc.scalar.activation(ident[:], zeros[:], RELU)
+        make_identity(nc, ident[:], nomemset=True)
+        for e in range(SCALE_BUFFERS):
+            gather_scales(e, e + 1, e)
+        for e in range(AHEAD):
+            gather_words(e)
+        load_w1_scales(FIRST_PLANES, PLANE_EXPERTS, nc.gpsimd)
+        for a in range(WEIGHT_RUN, E, WEIGHT_RUN):
+            load_w1_words(a)
+        nc.gpsimd.dma_start(w2w[:].bitcast(I32), w2_words.bitcast(I32).rearrange("e s p n -> p (e s) n"))
+        nc.gpsimd.dma_start(gate_last[:], gate[TOP - 1])
+        nc.gpsimd.dma_start(gate_rows[0 : (TOP - 1) * BLOCKS, :], gate[0 : TOP - 1, 0, :].rearrange("r (c m) -> r c m", m=P))
+
+        def refill_scales(e):
+            a = SCALE_BUFFERS + 2 * REFILL_AFTER.index(e)
+            gather_scales(a, a + 2, buffer_of[e])
+
+        for e in range(E):
+            layer1(e, 0)
+            layer1(e, 1)
+            if e >= 1:
+                turn(e - 1, (0, 1), t_bank[(e - 1) % T_BANKS])
+            if e == REFILL_AFTER[0]:
+                refill_scales(e)
+            if e + AHEAD < E:
+                gather_words(e + AHEAD)
+            if e in REFILL_AFTER[1:]:
+                refill_scales(e)
+            if e == E - PLANE_EXPERTS - 1:
+                load_w1_scales(PLANE_EXPERTS, E, nc.sync)
+                for r, pos in enumerate((pos1, pos2, pos3, pos4)):
+                    nc.sync.dma_start(pos_t[r][:], pos)
+            if e == 5:
+                load_w2_scales()
+        last = E - 1
+        turn(last, (0,), t_bank[1])
+        turn(last, (1,), t_bank[2])
+
         h_scales = keep.tile([P, S], U8, name="h_scales", align_bytes=64)
         h_late = keep.tile([P, S - EARLY], U32, name="h_late", align_bytes=64)
-        h_early = []
+        h_early = keep.tile([P, EARLY], U32, name="w1w6", align_bytes=64)
 
         def h_words(a, b):
-            return h_early[0][:, a:b] if a < EARLY else h_late[:, a - EARLY : b - EARLY]
-
-        def quantise(a, b):
-            nc.vector.quantize_mx(out=h_words(a, b).bitcast(FP8X4), scales=h_scales[:, a:b], in_=h_cols[:, 4 * a : 4 * b])
+            return h_early[:, a:b] if a < EARLY else h_late[:, a - EARLY : b - EARLY]
 
         def layer2(a, b, bank):
             step = min(C, b - a)
@@ -182,58 +218,18 @@ def tile_moe_pkd_mlp_relu_kernel(tc, x_words, x_scales, w1_words, w1_scales, w2_
                     stop=True,
                 )
 
-        load_w1_scales(0, 2, nc.sync)
-        load_w1_words(0, 3)
-        nc.scalar.activation(warm[:, 0:1], warm[:, 1:2], RELU)
-        make_identity(nc, ident[:], nomemset=True)
-        for c in range(4):
-            gather_scales(c)
-        for e in range(3):
-            gather_words(e)
-        load_w1_scales(2, SLOTS, nc.gpsimd)
-        load_w1_words(3, 6)
-        load_w1_words(6, 9)
-        load_w1_words(9, E)
-        load_w2()
-        nc.gpsimd.dma_start(gate_last[:], gate[TOP - 1])
-        nc.gpsimd.dma_start(gate_rows[0 : (TOP - 1) * BLOCKS, :], gate[0 : TOP - 1, 0, :].rearrange("r (c m) -> r c m", m=P))
-        for e in range(E):
-            layer1(e, 0)
-            layer1(e, 1)
-            if e >= 1:
-                turn(e - 1, (0, 1), t_bank[(e - 1) % T_BANKS])
-            if e == 0:
-                gather_scales(4)
-            if e + 3 < E:
-                gather_words(e + 3)
-            if e in (1, 3, 5):
-                gather_scales(5 + e // 2)
-            if e == 3:
-                load_w1_scales(SLOTS, E, nc.sync)
-            if e == 5:
-                load_w2_scales()
-            if e == 3:
-                for r, pos in enumerate((pos1, pos2, pos3, pos4)):
-                    nc.sync.dma_start(pos_t[r][:], pos)
-        last = E - 1
-        turn(last, (0,), t_bank[1])
-        turn(last, (1,), t_bank[2])
-        h_early.append(keep.tile([P, EARLY], U32, name="w1w6", align_bytes=64))
-        for a in range(0, (E - 2) * C, 2 * C):
-            quantise(a, a + 2 * C)
         pieces = [
             (0, 2 * C, a_bank[0], True),
             (2 * C, 4 * C, t_bank[4], True),
             (4 * C, 6 * C, a_bank[1], False),
             (6 * C, 8 * C, a_bank[2], False),
             (8 * C, 10 * C, t_bank[0], False),
-            (10 * C, 11 * C, t_bank[3], False),
-            (11 * C, 11 * C + P, t_bank[1], True),
-            (11 * C + P, S, t_bank[2], True),
+            (10 * C, last * C, t_bank[3], False),
+            (last * C, last * C + P, t_bank[1], True),
+            (last * C + P, S, t_bank[2], True),
         ]
         for a, b, bank, on_vector in pieces:
-            if a >= (E - 2) * C:
-                quantise(a, b)
+            nc.vector.quantize_mx(out=h_words(a, b).bitcast(FP8X4), scales=h_scales[:, a:b], in_=h_cols[:, 4 * a : 4 * b])
         for a, b, bank, on_vector in pieces:
             layer2(a, b, bank)
             if on_vector:
@@ -248,7 +244,7 @@ def tile_moe_pkd_mlp_relu_kernel(tc, x_words, x_scales, w1_words, w1_scales, w2_
         scaled = keep.tile([P, TOP - 1, T], F32, name="scaled")
         prod = keep.tile([P, T], F32, name="prod")
         total = keep.tile([P, T], F32, name="total")
-        fwd_banks = [t_bank[4], a_bank[1], a_bank[2], a_bank[0]]
+        token_banks = [t_bank[4], a_bank[1], a_bank[2], a_bank[0]]
         sum_banks = [t_bank[0], t_bank[3], t_bank[1], t_bank[2]]
         per_half = HALF // P
 
@@ -257,37 +253,37 @@ def tile_moe_pkd_mlp_relu_kernel(tc, x_words, x_scales, w1_words, w1_scales, w2_
                 return sum_banks[0][:, c * P : (c + 1) * P]
             return sum_banks[1 + c - per_half][:, 0:P]
 
-        def back(r, c):
+        def add_back(r, c):
             nc.tensor.matmul(sum_place(c), lhsT=scaled[:, r, c * P : (c + 1) * P], rhs=ident[:], is_transpose=True, start=(r == 0), stop=(r == TOP - 2))
 
-        for hf in range(2):
-            a = hf * HALF
+        for side in range(2):
+            a = side * HALF
+            blocks = range(side * per_half, (side + 1) * per_half)
             for r in range(TOP - 1):
                 nc.vector.tensor_copy(picked[:, r, a : a + HALF], y_all[:].indirect(pos_t[r][:, a // 16 : (a + HALF) // 16]))
-                bank = fwd_banks[(hf * (TOP - 1) + r) % len(fwd_banks)]
-                blocks = range(hf * per_half, (hf + 1) * per_half)
+                bank = token_banks[(side * (TOP - 1) + r) % len(token_banks)]
                 for j, c in enumerate(blocks):
                     nc.tensor.transpose(bank[:, j * P : (j + 1) * P], picked[:, r, c * P : (c + 1) * P], ident[:])
                 for j, c in enumerate(blocks):
                     nc.scalar.activation(scaled[:, r, c * P : (c + 1) * P], bank[:, j * P : (j + 1) * P], COPY, scale=gate_cols[:, r * BLOCKS + c : r * BLOCKS + c + 1])
-                if hf == 1:
+                if side == 1:
                     for c in blocks:
-                        back(r, c)
-            if hf == 0:
-                for c in range(per_half):
+                        add_back(r, c)
+            if side == 0:
+                for c in blocks:
                     for r in range(TOP - 1):
-                        back(r, c)
+                        add_back(r, c)
 
         def last_choice(a, b):
             nc.vector.tensor_tensor(prod[:, a:b], y_all[:].indirect(pos_t[TOP - 1][:, a // 16 : b // 16]), gate_last[:, a:b], MULT)
 
         last_choice(0, HALF)
-        last_choice(HALF, HALF + 2 * P)
+        last_choice(HALF, T - P)
         nc.vector.tensor_tensor(total[:, 0:HALF], prod[:, 0:HALF], sum_banks[0][:, 0:HALF], ADD)
         nc.sync.dma_start(out[:, 0:HALF], total[:, 0:HALF])
-        last_choice(HALF + 2 * P, T)
+        last_choice(T - P, T)
         for c in range(per_half, BLOCKS):
             nc.vector.tensor_tensor(total[:, c * P : (c + 1) * P], prod[:, c * P : (c + 1) * P], sum_place(c), ADD)
             if c == BLOCKS - 2:
-                nc.sync.dma_start(out[:, HALF : HALF + 2 * P], total[:, HALF : HALF + 2 * P])
+                nc.sync.dma_start(out[:, HALF : T - P], total[:, HALF : T - P])
         nc.sync.dma_start(out[:, T - P : T], total[:, T - P : T])

@@ -28,8 +28,6 @@ REFILL_AFTER = (0, 1, 3, 5)
 PLANE_EXPERTS = 8
 FIRST_PLANES = 2
 WEIGHT_RUN = 3
-A_BANKS = 3
-T_BANKS = 5
 EARLY = 6 * C
 BLOCKS = T // P
 HALF = T // 2
@@ -46,8 +44,11 @@ def tile_moe_pkd_mlp_relu_kernel(tc, x_words, x_scales, w1_words, w1_scales, w2_
 
         offs_t = lists.tile([P, S // 16], U16, name="offs_t")
         pos_t = [lists.tile([P, T // 16], U16, name="pos_t%d" % r) for r in range(TOP)]
-        a_bank = [psum.tile([P, H], F32, name="a_bank%d" % b) for b in range(A_BANKS)]
-        t_bank = [psum.tile([P, H], F32, name="t_bank%d" % b) for b in range(T_BANKS)]
+        banks = [psum.tile([P, H], F32, name="bank%d" % b) for b in range(8)]
+
+        def sum_bank(e, half):
+            return banks[2 * ((e // 2 + e % 2) % 2) + half]
+
 
         xs = keep.tile([P, T], U8, name="xs", align_bytes=64)
         xw = keep.tile([P, 2, T], U32, name="xw", align_bytes=64)
@@ -127,7 +128,7 @@ def tile_moe_pkd_mlp_relu_kernel(tc, x_words, x_scales, w1_words, w1_scales, w2_
         h_rows = {}
 
         def layer1(e, half):
-            acc = a_bank[(2 * e + half) % A_BANKS]
+            acc = sum_bank(e, half)
             for o in range(2):
                 nc.tensor.matmul_mx(
                     out=acc[:],
@@ -179,8 +180,14 @@ def tile_moe_pkd_mlp_relu_kernel(tc, x_words, x_scales, w1_words, w1_scales, w2_
         for e in range(E):
             layer1(e, 0)
             layer1(e, 1)
-            if e >= 1:
-                turn(e - 1, (0, 1), t_bank[(e - 1) % T_BANKS])
+            if e == E - 2:
+                turn(e - 1, (0, 1), banks[4])
+            elif e == E - 1:
+                turn(e - 1, (0, 1), banks[5])
+            elif e % 2 == 1:
+                if e > 1:
+                    turn(e - 2, (0, 1), sum_bank(e - 1, 0))
+                turn(e - 1, (0, 1), sum_bank(e - 1, 1))
             if e == REFILL_AFTER[0]:
                 refill_scales(e)
             if e + AHEAD < E:
@@ -194,8 +201,8 @@ def tile_moe_pkd_mlp_relu_kernel(tc, x_words, x_scales, w1_words, w1_scales, w2_
             if e == 5:
                 load_w2_scales()
         last = E - 1
-        turn(last, (0,), t_bank[1])
-        turn(last, (1,), t_bank[2])
+        turn(last, (0,), banks[6])
+        turn(last, (1,), banks[7])
 
         h_scales = keep.tile([P, S], U8, name="h_scales", align_bytes=64)
         h_late = keep.tile([P, S - EARLY], U32, name="h_late", align_bytes=64)
@@ -219,14 +226,14 @@ def tile_moe_pkd_mlp_relu_kernel(tc, x_words, x_scales, w1_words, w1_scales, w2_
                 )
 
         pieces = [
-            (0, 2 * C, a_bank[0], True),
-            (2 * C, 4 * C, t_bank[4], True),
-            (4 * C, 6 * C, a_bank[1], False),
-            (6 * C, 8 * C, a_bank[2], False),
-            (8 * C, 10 * C, t_bank[0], False),
-            (10 * C, last * C, t_bank[3], False),
-            (last * C, last * C + P, t_bank[1], True),
-            (last * C + P, S, t_bank[2], True),
+            (0, 2 * C, sum_bank(10, 0), True),
+            (2 * C, 4 * C, sum_bank(10, 1), True),
+            (4 * C, 6 * C, sum_bank(11, 0), False),
+            (6 * C, 8 * C, sum_bank(11, 1), False),
+            (8 * C, 10 * C, banks[4], False),
+            (10 * C, last * C, banks[5], False),
+            (last * C, last * C + P, banks[6], True),
+            (last * C + P, S, banks[7], True),
         ]
         for a, b, bank, on_vector in pieces:
             nc.vector.quantize_mx(out=h_words(a, b).bitcast(FP8X4), scales=h_scales[:, a:b], in_=h_cols[:, 4 * a : 4 * b])
@@ -237,15 +244,15 @@ def tile_moe_pkd_mlp_relu_kernel(tc, x_words, x_scales, w1_words, w1_scales, w2_
             else:
                 nc.scalar.copy(y_all[:, a:b], bank[:, 0 : b - a])
 
-        nc.tensor.transpose(a_bank[0][:, 0:P], gate_rows[:], ident[:])
-        nc.scalar.copy(gate_cols[:, 0 : (TOP - 1) * BLOCKS], a_bank[0][:, 0 : (TOP - 1) * BLOCKS])
+        nc.tensor.transpose(sum_bank(10, 0)[:, 0:P], gate_rows[:], ident[:])
+        nc.scalar.copy(gate_cols[:, 0 : (TOP - 1) * BLOCKS], sum_bank(10, 0)[:, 0 : (TOP - 1) * BLOCKS])
 
         picked = keep.tile([P, TOP - 1, T], F32, name="picked")
         scaled = keep.tile([P, TOP - 1, T], F32, name="scaled")
         prod = keep.tile([P, T], F32, name="prod")
         total = keep.tile([P, T], F32, name="total")
-        token_banks = [t_bank[4], a_bank[1], a_bank[2], a_bank[0]]
-        sum_banks = [t_bank[0], t_bank[3], t_bank[1], t_bank[2]]
+        token_banks = [sum_bank(10, 1), sum_bank(11, 0), sum_bank(11, 1), sum_bank(10, 0)]
+        sum_banks = banks[4:8]
         per_half = HALF // P
 
         def sum_place(c):

@@ -30,7 +30,8 @@ FIRST_PLANES = 2
 WEIGHT_RUN = 3
 EARLY = 6 * C
 BLOCKS = T // P
-HALF = T // 2
+BOTH = 5
+SPLIT = BOTH * P
 
 
 def tile_moe_pkd_mlp_relu_kernel(tc, x_words, x_scales, w1_words, w1_scales, w2_words, w2_scales, gate, offs, pos1, pos2, pos3, pos4, out):
@@ -95,7 +96,7 @@ def tile_moe_pkd_mlp_relu_kernel(tc, x_words, x_scales, w1_words, w1_scales, w2_
                 dst = w2s[32 * q : 32 * q + 4, 0 : E * N].bitcast(I32).rearrange("p (e n) -> p e n", e=E)
                 nc.sync.dma_start(dst, src[4 * q : 4 * q + 4, :, :])
 
-        gate_last = keep.tile([P, T], F32, name="gate_last")
+        gate_planes = keep.tile([P, 2, T], F32, name="gate_planes")
         gate_rows = keep.tile([P, P], F32, name="gate_rows")
         gate_cols = keep.tile([P, P], F32, name="gate_cols")
         nc.vector.memset(gate_rows[:], 0.0)
@@ -170,8 +171,8 @@ def tile_moe_pkd_mlp_relu_kernel(tc, x_words, x_scales, w1_words, w1_scales, w2_
         for a in range(WEIGHT_RUN, E, WEIGHT_RUN):
             load_w1_words(a)
         nc.gpsimd.dma_start(w2w[:].bitcast(I32), w2_words.bitcast(I32).rearrange("e s p n -> p (e s) n"))
-        nc.gpsimd.dma_start(gate_last[:], gate[TOP - 1])
-        nc.gpsimd.dma_start(gate_rows[0 : (TOP - 1) * BLOCKS, :], gate[0 : TOP - 1, 0, :].rearrange("r (c m) -> r c m", m=P))
+        nc.gpsimd.dma_start(gate_planes[:], gate[2:TOP].rearrange("r p t -> p r t"))
+        nc.gpsimd.dma_start(gate_rows[0 : 2 * BLOCKS, :], gate[0:2, 0, :].rearrange("r (c m) -> r c m", m=P))
 
         def refill_scales(e):
             a = SCALE_BUFFERS + 2 * REFILL_AFTER.index(e)
@@ -200,6 +201,8 @@ def tile_moe_pkd_mlp_relu_kernel(tc, x_words, x_scales, w1_words, w1_scales, w2_
                     nc.sync.dma_start(pos_t[r][:], pos)
             if e == 5:
                 load_w2_scales()
+        gate_rest = keep.tile([P, T - SPLIT], F32, name="w1w0", align_bytes=64)
+        nc.sync.dma_start(gate_rest[:], gate[1, :, SPLIT:T])
         last = E - 1
         turn(last, (0,), banks[6])
         turn(last, (1,), banks[7])
@@ -231,7 +234,7 @@ def tile_moe_pkd_mlp_relu_kernel(tc, x_words, x_scales, w1_words, w1_scales, w2_
             (4 * C, 6 * C, sum_bank(11, 0), False),
             (6 * C, 8 * C, sum_bank(11, 1), False),
             (8 * C, 10 * C, banks[4], False),
-            (10 * C, last * C, banks[5], False),
+            (10 * C, last * C, banks[5], True),
             (last * C, last * C + P, banks[6], True),
             (last * C + P, S, banks[7], True),
         ]
@@ -245,52 +248,59 @@ def tile_moe_pkd_mlp_relu_kernel(tc, x_words, x_scales, w1_words, w1_scales, w2_
                 nc.scalar.copy(y_all[:, a:b], bank[:, 0 : b - a])
 
         nc.tensor.transpose(sum_bank(10, 0)[:, 0:P], gate_rows[:], ident[:])
-        nc.scalar.copy(gate_cols[:, 0 : (TOP - 1) * BLOCKS], sum_bank(10, 0)[:, 0 : (TOP - 1) * BLOCKS])
+        nc.scalar.copy(gate_cols[:, 0 : 2 * BLOCKS], sum_bank(10, 0)[:, 0 : 2 * BLOCKS])
 
-        picked = keep.tile([P, TOP - 1, T], F32, name="picked")
-        scaled = keep.tile([P, TOP - 1, T], F32, name="scaled")
-        prod = keep.tile([P, T], F32, name="prod")
+        picked = keep.tile([P, 2, T], F32, name="picked")
+        scaled = keep.tile([P, 2, T], F32, name="scaled")
+        prod = keep.tile([P, 2, T], F32, name="prod")
+        prod_rest = keep.tile([P, T - SPLIT], F32, name="prod_rest")
+        part_rest = keep.tile([P, T - SPLIT], F32, name="part_rest")
+        pair = keep.tile([P, T], F32, name="pair")
         total = keep.tile([P, T], F32, name="total")
-        token_banks = [sum_bank(10, 1), sum_bank(11, 0), sum_bank(11, 1), sum_bank(10, 0)]
-        sum_banks = banks[4:8]
-        per_half = HALF // P
 
-        def sum_place(c):
-            if c < per_half:
-                return sum_banks[0][:, c * P : (c + 1) * P]
-            return sum_banks[1 + c - per_half][:, 0:P]
+        def pick(r, a, b, bank):
+            nc.scalar.activation(picked[:, r, a:b], y_all[:].indirect(pos_t[r][:, a // 16 : b // 16]), COPY)
+            for j in range(a, b, P):
+                nc.tensor.transpose(bank[:, j - a : j - a + P], picked[:, r, j : j + P], ident[:])
 
-        def add_back(r, c):
-            nc.tensor.matmul(sum_place(c), lhsT=scaled[:, r, c * P : (c + 1) * P], rhs=ident[:], is_transpose=True, start=(r == 0), stop=(r == TOP - 2))
+        def weigh(r, a, b, bank):
+            for j in range(a, b, P):
+                column = r * BLOCKS + j // P
+                nc.scalar.activation(scaled[:, r, j : j + P], bank[:, j - a : j - a + P], COPY, scale=gate_cols[:, column : column + 1])
 
-        for side in range(2):
-            a = side * HALF
-            blocks = range(side * per_half, (side + 1) * per_half)
-            for r in range(TOP - 1):
-                nc.vector.tensor_copy(picked[:, r, a : a + HALF], y_all[:].indirect(pos_t[r][:, a // 16 : (a + HALF) // 16]))
-                bank = token_banks[(side * (TOP - 1) + r) % len(token_banks)]
-                for j, c in enumerate(blocks):
-                    nc.tensor.transpose(bank[:, j * P : (j + 1) * P], picked[:, r, c * P : (c + 1) * P], ident[:])
-                for j, c in enumerate(blocks):
-                    nc.scalar.activation(scaled[:, r, c * P : (c + 1) * P], bank[:, j * P : (j + 1) * P], COPY, scale=gate_cols[:, r * BLOCKS + c : r * BLOCKS + c + 1])
-                if side == 1:
-                    for c in blocks:
-                        add_back(r, c)
-            if side == 0:
-                for c in blocks:
-                    for r in range(TOP - 1):
-                        add_back(r, c)
+        def add_back(j, place, choices):
+            for r in range(choices):
+                nc.tensor.matmul(place, lhsT=scaled[:, r, j : j + P], rhs=ident[:], is_transpose=True, start=(r == 0), stop=(r == choices - 1))
 
-        def last_choice(a, b):
-            nc.vector.tensor_tensor(prod[:, a:b], y_all[:].indirect(pos_t[TOP - 1][:, a // 16 : b // 16]), gate_last[:, a:b], MULT)
+        def fused(dst, r, a, b, weights):
+            nc.vector.tensor_tensor(dst, y_all[:].indirect(pos_t[r][:, a // 16 : b // 16]), weights, MULT)
 
-        last_choice(0, HALF)
-        last_choice(HALF, T - P)
-        nc.vector.tensor_tensor(total[:, 0:HALF], prod[:, 0:HALF], sum_banks[0][:, 0:HALF], ADD)
-        nc.sync.dma_start(out[:, 0:HALF], total[:, 0:HALF])
-        last_choice(T - P, T)
-        for c in range(per_half, BLOCKS):
-            nc.vector.tensor_tensor(total[:, c * P : (c + 1) * P], prod[:, c * P : (c + 1) * P], sum_place(c), ADD)
-            if c == BLOCKS - 2:
-                nc.sync.dma_start(out[:, HALF : T - P], total[:, HALF : T - P])
-        nc.sync.dma_start(out[:, T - P : T], total[:, T - P : T])
+        first = 3 * P
+        last_block = SPLIT - P
+        pick(0, first, T, sum_bank(10, 1))
+        pick(0, 0, first, sum_bank(11, 0))
+        pick(1, 0, first, sum_bank(11, 1))
+        pick(1, first, SPLIT, sum_bank(10, 0))
+        weigh(0, first, T, sum_bank(10, 1))
+        add_back(SPLIT, banks[4][:, 0:P], 1)
+        weigh(0, 0, first, sum_bank(11, 0))
+        weigh(1, 0, first, sum_bank(11, 1))
+        for j in range(0, first, P):
+            add_back(j, banks[5][:, j : j + P], 2)
+        weigh(1, first, SPLIT, sum_bank(10, 0))
+        add_back(first, banks[7][:, 0:P], 2)
+        add_back(last_block, banks[6][:, 0:P], 2)
+
+        fused(prod_rest[:], 1, SPLIT, T, gate_rest[:])
+        fused(prod[:, 0, :], 2, 0, T, gate_planes[:, 0, :])
+        fused(prod[:, 1, :], 3, 0, T, gate_planes[:, 1, :])
+        nc.vector.tensor_tensor(part_rest[:], prod_rest[:], prod[:, 0, SPLIT:T], ADD)
+        nc.vector.tensor_tensor(pair[:, 0:SPLIT], prod[:, 0, 0:SPLIT], prod[:, 1, 0:SPLIT], ADD)
+        nc.vector.tensor_tensor(pair[:, SPLIT:T], part_rest[:], prod[:, 1, SPLIT:T], ADD)
+        nc.vector.tensor_tensor(total[:, SPLIT:T], pair[:, SPLIT:T], banks[4][:, 0 : T - SPLIT], ADD)
+        nc.sync.dma_start(out[:, SPLIT:T], total[:, SPLIT:T])
+        nc.vector.tensor_tensor(total[:, 0:first], pair[:, 0:first], banks[5][:, 0:first], ADD)
+        nc.sync.dma_start(out[:, 0:first], total[:, 0:first])
+        nc.vector.tensor_tensor(total[:, first:last_block], pair[:, first:last_block], banks[7][:, 0:P], ADD)
+        nc.vector.tensor_tensor(total[:, last_block:SPLIT], pair[:, last_block:SPLIT], banks[6][:, 0:P], ADD)
+        nc.sync.dma_start(out[:, first:SPLIT], total[:, first:SPLIT])

@@ -27,7 +27,7 @@ SCALE_BUFFERS = 4
 REFILL_AFTER = (0, 1, 3, 5)
 PLANE_EXPERTS = 8
 FIRST_PLANES = 2
-WEIGHT_RUN = 3
+WEIGHT_RUNS = ((0, 2), (2, 5), (5, 9), (9, 12))
 EARLY = 6 * C
 BLOCKS = T // P
 BOTH = 5
@@ -81,9 +81,8 @@ def tile_moe_pkd_mlp_relu_kernel(tc, x_words, x_scales, w1_words, w1_scales, w2_
 
         w1w = {}
 
-        def load_w1_words(a):
-            b = a + WEIGHT_RUN
-            words = keep.tile([P, 2 * WEIGHT_RUN, 2 * H], U8, name="w1w%d" % a, align_bytes=64)
+        def load_w1_words(a, b):
+            words = keep.tile([P, 2 * (b - a), 2 * H], U8, name="w1w%d" % a, align_bytes=64)
             nc.gpsimd.dma_start(words[:].bitcast(I32), w1_words[a:b].bitcast(I32).rearrange("e s p n -> p (e s) n"))
             for e in range(a, b):
                 w1w[e] = words[:, 2 * (e - a) : 2 * (e - a) + 2, :]
@@ -148,7 +147,7 @@ def tile_moe_pkd_mlp_relu_kernel(tc, x_words, x_scales, w1_words, w1_scales, w2_
 
         h_cols = keep.tile([P, 4 * S], BF16, name="h_cols", align_bytes=64)
 
-        def turn(e, halves, bank):
+        def turn(e, halves, bank, on_vector=False):
             count = len(halves)
             turned = bank[:, 0 : count * 2 * P].rearrange("p (a u j) -> p a u j", a=count, u=2)
             for a, half in enumerate(halves):
@@ -157,10 +156,14 @@ def tile_moe_pkd_mlp_relu_kernel(tc, x_words, x_scales, w1_words, w1_scales, w2_
                     nc.tensor.transpose(turned[:, a, u, :], pairs[:, u * P : (u + 1) * P], ident[:])
             first = e * C + halves[0] * P
             dst = h_cols[:, 4 * first : 4 * (first + count * P)].bitcast(F32).rearrange("p (a j u) -> p a j u", a=count, u=2)
-            nc.scalar.copy(dst, turned.rearrange("p a u j -> p a j u"))
+            src = turned.rearrange("p a u j -> p a j u")
+            if on_vector:
+                nc.vector.tensor_copy(dst, src)
+            else:
+                nc.scalar.copy(dst, src)
 
         load_w1_scales(0, FIRST_PLANES, nc.sync)
-        load_w1_words(0)
+        load_w1_words(*WEIGHT_RUNS[0])
         nc.scalar.activation(ident[:], zeros[:], RELU)
         make_identity(nc, ident[:], nomemset=True)
         for e in range(SCALE_BUFFERS):
@@ -168,8 +171,8 @@ def tile_moe_pkd_mlp_relu_kernel(tc, x_words, x_scales, w1_words, w1_scales, w2_
         for e in range(AHEAD):
             gather_words(e)
         load_w1_scales(FIRST_PLANES, PLANE_EXPERTS, nc.gpsimd)
-        for a in range(WEIGHT_RUN, E, WEIGHT_RUN):
-            load_w1_words(a)
+        for a, b in WEIGHT_RUNS[1:]:
+            load_w1_words(a, b)
         nc.gpsimd.dma_start(w2w[:].bitcast(I32), w2_words.bitcast(I32).rearrange("e s p n -> p (e s) n"))
         nc.gpsimd.dma_start(gate_planes[:], gate[2:TOP].rearrange("r p t -> p r t"))
         nc.gpsimd.dma_start(gate_rows[0 : 2 * BLOCKS, :], gate[0:2, 0, :].rearrange("r (c m) -> r c m", m=P))
@@ -182,9 +185,9 @@ def tile_moe_pkd_mlp_relu_kernel(tc, x_words, x_scales, w1_words, w1_scales, w2_
             layer1(e, 0)
             layer1(e, 1)
             if e == E - 2:
-                turn(e - 1, (0, 1), banks[4])
+                turn(e - 1, (0, 1), banks[4], on_vector=True)
             elif e == E - 1:
-                turn(e - 1, (0, 1), banks[5])
+                turn(e - 1, (0, 1), banks[5], on_vector=True)
             elif e % 2 == 1:
                 if e > 1:
                     turn(e - 2, (0, 1), sum_bank(e - 1, 0))
@@ -209,7 +212,7 @@ def tile_moe_pkd_mlp_relu_kernel(tc, x_words, x_scales, w1_words, w1_scales, w2_
 
         h_scales = keep.tile([P, S], U8, name="h_scales", align_bytes=64)
         h_late = keep.tile([P, S - EARLY], U32, name="h_late", align_bytes=64)
-        h_early = keep.tile([P, EARLY], U32, name="w1w6", align_bytes=64)
+        h_early = keep.tile([P, EARLY], U32, name="w1w5", align_bytes=64)
 
         def h_words(a, b):
             return h_early[:, a:b] if a < EARLY else h_late[:, a - EARLY : b - EARLY]
@@ -229,11 +232,11 @@ def tile_moe_pkd_mlp_relu_kernel(tc, x_words, x_scales, w1_words, w1_scales, w2_
                 )
 
         pieces = [
-            (0, 2 * C, sum_bank(10, 0), True),
-            (2 * C, 4 * C, sum_bank(10, 1), True),
+            (0, 2 * C, sum_bank(10, 0), False),
+            (2 * C, 4 * C, sum_bank(10, 1), False),
             (4 * C, 6 * C, sum_bank(11, 0), False),
             (6 * C, 8 * C, sum_bank(11, 1), False),
-            (8 * C, 10 * C, banks[4], False),
+            (8 * C, 10 * C, banks[4], True),
             (10 * C, last * C, banks[5], True),
             (last * C, last * C + P, banks[6], True),
             (last * C + P, S, banks[7], True),

@@ -47,8 +47,11 @@ def tile_moe_pkd_mlp_relu_kernel(tc, x_words, x_scales, w1_words, w1_scales, w2_
         pos_t = [lists.tile([P, T // 16], U16, name="pos_t%d" % r) for r in range(TOP)]
         banks = [psum.tile([P, H], F32, name="bank%d" % b) for b in range(8)]
 
+        spare = banks[0:4]
+
         def sum_bank(e, half):
-            return banks[2 * ((e // 2 + e % 2) % 2) + half]
+            pairs = spare if e < 2 else banks[4:8]
+            return pairs[2 * ((e // 2 + e % 2) % 2) + half]
 
 
         xs = keep.tile([P, T], U8, name="xs", align_bytes=64)
@@ -129,15 +132,16 @@ def tile_moe_pkd_mlp_relu_kernel(tc, x_words, x_scales, w1_words, w1_scales, w2_
 
         def layer1(e, half):
             acc = sum_bank(e, half)
-            for o in range(2):
+            order = (1, 0) if e in (1, 2, 3) else (0, 1)
+            for o in order:
                 nc.tensor.matmul_mx(
                     out=acc[:],
                     lhsT=slot_words[(e, o)][:, half * P : (half + 1) * P].bitcast(FP8X4),
                     lhsT_scale=slot_scales[e * C + half * P][o],
                     rhs=w1w[e][:, o, :].bitcast(FP4X4),
                     rhs_scale=plane[:, 2 * (e % PLANE_EXPERTS) + o, :],
-                    start=(o == 0),
-                    stop=(o == 1),
+                    start=(o == order[0]),
+                    stop=(o == order[1]),
                 )
             hr = hring.tile([P, H], BF16, name="hr")
             dst = hr[:].rearrange("j (u p d) -> j u p d", u=2, d=2)
@@ -185,9 +189,9 @@ def tile_moe_pkd_mlp_relu_kernel(tc, x_words, x_scales, w1_words, w1_scales, w2_
             layer1(e, 0)
             layer1(e, 1)
             if e == E - 2:
-                turn(e - 1, (0, 1), banks[4], on_vector=True)
+                turn(e - 1, (0, 1), spare[0], on_vector=True)
             elif e == E - 1:
-                turn(e - 1, (0, 1), banks[5], on_vector=True)
+                turn(e - 1, (0, 1), spare[1], on_vector=True)
             elif e % 2 == 1:
                 if e > 1:
                     turn(e - 2, (0, 1), sum_bank(e - 1, 0))
@@ -207,8 +211,8 @@ def tile_moe_pkd_mlp_relu_kernel(tc, x_words, x_scales, w1_words, w1_scales, w2_
         gate_rest = keep.tile([P, T - SPLIT], F32, name="w1w0", align_bytes=64)
         nc.sync.dma_start(gate_rest[:], gate[1, :, SPLIT:T])
         last = E - 1
-        turn(last, (0,), banks[6])
-        turn(last, (1,), banks[7])
+        turn(last, (0,), spare[2])
+        turn(last, (1,), spare[3])
 
         h_scales = keep.tile([P, S], U8, name="h_scales", align_bytes=64)
         h_late = keep.tile([P, S - EARLY], U32, name="h_late", align_bytes=64)
@@ -236,10 +240,10 @@ def tile_moe_pkd_mlp_relu_kernel(tc, x_words, x_scales, w1_words, w1_scales, w2_
             (2 * C, 4 * C, sum_bank(10, 1), False),
             (4 * C, 6 * C, sum_bank(11, 0), False),
             (6 * C, 8 * C, sum_bank(11, 1), False),
-            (8 * C, 10 * C, banks[4], True),
-            (10 * C, last * C, banks[5], True),
-            (last * C, last * C + P, banks[6], True),
-            (last * C + P, S, banks[7], True),
+            (8 * C, 10 * C, spare[0], True),
+            (10 * C, last * C, spare[1], True),
+            (last * C, last * C + P, spare[2], True),
+            (last * C + P, S, spare[3], True),
         ]
         for a, b, bank, on_vector in pieces:
             nc.vector.quantize_mx(out=h_words(a, b).bitcast(FP8X4), scales=h_scales[:, a:b], in_=h_cols[:, 4 * a : 4 * b])
@@ -280,19 +284,19 @@ def tile_moe_pkd_mlp_relu_kernel(tc, x_words, x_scales, w1_words, w1_scales, w2_
 
         first = 3 * P
         last_block = SPLIT - P
-        pick(0, first, T, sum_bank(10, 1))
-        pick(0, 0, first, sum_bank(11, 0))
-        pick(1, 0, first, sum_bank(11, 1))
+        pick(0, 0, first, sum_bank(10, 1))
+        pick(1, 0, first, sum_bank(11, 0))
+        pick(0, first, T, sum_bank(11, 1))
         pick(1, first, SPLIT, sum_bank(10, 0))
-        weigh(0, first, T, sum_bank(10, 1))
-        add_back(SPLIT, banks[4][:, 0:P], 1)
-        weigh(0, 0, first, sum_bank(11, 0))
-        weigh(1, 0, first, sum_bank(11, 1))
+        weigh(0, 0, first, sum_bank(10, 1))
+        weigh(1, 0, first, sum_bank(11, 0))
         for j in range(0, first, P):
-            add_back(j, banks[5][:, j : j + P], 2)
+            add_back(j, spare[1][:, j : j + P], 2)
+        weigh(0, first, T, sum_bank(11, 1))
+        add_back(SPLIT, spare[0][:, 0:P], 1)
         weigh(1, first, SPLIT, sum_bank(10, 0))
-        add_back(first, banks[7][:, 0:P], 2)
-        add_back(last_block, banks[6][:, 0:P], 2)
+        add_back(first, spare[3][:, 0:P], 2)
+        add_back(last_block, spare[2][:, 0:P], 2)
 
         fused(prod_rest[:], 1, SPLIT, T, gate_rest[:])
         fused(prod[:, 0, :], 2, 0, T, gate_planes[:, 0, :])
@@ -300,10 +304,10 @@ def tile_moe_pkd_mlp_relu_kernel(tc, x_words, x_scales, w1_words, w1_scales, w2_
         nc.vector.tensor_tensor(part_rest[:], prod_rest[:], prod[:, 0, SPLIT:T], ADD)
         nc.vector.tensor_tensor(pair[:, 0:SPLIT], prod[:, 0, 0:SPLIT], prod[:, 1, 0:SPLIT], ADD)
         nc.vector.tensor_tensor(pair[:, SPLIT:T], part_rest[:], prod[:, 1, SPLIT:T], ADD)
-        nc.vector.tensor_tensor(total[:, SPLIT:T], pair[:, SPLIT:T], banks[4][:, 0 : T - SPLIT], ADD)
-        nc.sync.dma_start(out[:, SPLIT:T], total[:, SPLIT:T])
-        nc.vector.tensor_tensor(total[:, 0:first], pair[:, 0:first], banks[5][:, 0:first], ADD)
+        nc.vector.tensor_tensor(total[:, 0:first], pair[:, 0:first], spare[1][:, 0:first], ADD)
         nc.sync.dma_start(out[:, 0:first], total[:, 0:first])
-        nc.vector.tensor_tensor(total[:, first:last_block], pair[:, first:last_block], banks[7][:, 0:P], ADD)
-        nc.vector.tensor_tensor(total[:, last_block:SPLIT], pair[:, last_block:SPLIT], banks[6][:, 0:P], ADD)
+        nc.vector.tensor_tensor(total[:, SPLIT:T], pair[:, SPLIT:T], spare[0][:, 0 : T - SPLIT], ADD)
+        nc.sync.dma_start(out[:, SPLIT:T], total[:, SPLIT:T])
+        nc.vector.tensor_tensor(total[:, first:last_block], pair[:, first:last_block], spare[3][:, 0:P], ADD)
+        nc.vector.tensor_tensor(total[:, last_block:SPLIT], pair[:, last_block:SPLIT], spare[2][:, 0:P], ADD)
         nc.sync.dma_start(out[:, first:SPLIT], total[:, first:SPLIT])

from contextlib import ExitStack

import concourse.mybir as mybir
from concourse.masks import make_identity

K, T, E, C, H, N = 1024, 768, 12, 256, 512, 128
TOP = 4
S = E * C
P = 128
FLOPS = 2 * S * (K * H + H * N)

F32 = mybir.dt.float32
BF16 = mybir.dt.bfloat16
I32 = mybir.dt.int32
U32 = mybir.dt.uint32
U16 = mybir.dt.uint16
U8 = mybir.dt.uint8
FP8X4 = mybir.dt.float8_e4m3fn_x4
FP4X4 = mybir.dt.float4_e2m1fn_x4
RELU = mybir.ActivationFunctionType.Relu
COPY = mybir.ActivationFunctionType.Copy
MULT = mybir.AluOpType.mult
ADD = mybir.AluOpType.add

AHEAD = 3
SCALE_BUFFERS = 4
REFILL_AFTER = (0, 1, 3, 5)
PLANE_EXPERTS = 8
FIRST_PLANES = 2
WEIGHT_RUNS = ((0, 2), (2, 5), (5, 9), (9, 12))
EARLY = 6 * C
BLOCKS = T // P
BOTH = 5
SPLIT = BOTH * P


def tile_moe_pkd_mlp_relu_kernel(tc, x_words, x_scales, w1_words, w1_scales, w2_words, w2_scales, gate, offs, pos1, pos2, pos3, pos4, out):
    nc = tc.nc
    with ExitStack() as ctx:
        lists = ctx.enter_context(tc.tile_pool(name="lists", bufs=1))
        keep = ctx.enter_context(tc.tile_pool(name="keep", bufs=1))
        gring = ctx.enter_context(tc.tile_pool(name="gring", bufs=AHEAD))
        hring = ctx.enter_context(tc.tile_pool(name="hring", bufs=2 * AHEAD))
        psum = ctx.enter_context(tc.psum_pool(name="psum", bufs=1))

        offs_t = lists.tile([P, S // 16], U16, name="offs_t")
        pos_t = [lists.tile([P, T // 16], U16, name="pos_t%d" % r) for r in range(TOP)]
        banks = [psum.tile([P, H], F32, name="bank%d" % b) for b in range(8)]

        spare = banks[0:4]

        def sum_bank(e, half):
            pairs = spare if e < 2 else banks[4:8]
            return pairs[2 * ((e // 2 + e % 2) % 2) + half]


        xs = keep.tile([P, T], U8, name="xs", align_bytes=64)
        xw = keep.tile([P, 2, T], U32, name="xw", align_bytes=64)
        plane = keep.tile([P, 2 * PLANE_EXPERTS, H], U8, name="plane", align_bytes=64)
        y_all = keep.tile([P, S], F32, name="y_all")
        ident = keep.tile([P, P], F32, name="ident")
        zeros = keep.tile([P, P], F32, name="zeros")

        gathered = keep.tile([P, SCALE_BUFFERS, 2 * C], U8, name="gathered", align_bytes=64)
        shifted = keep.tile([P, SCALE_BUFFERS, 2 * C], U8, name="shifted", align_bytes=64)
        w2w = keep.tile([P, E, 2 * N], U8, name="w2w", align_bytes=64)
        nc.vector.memset(plane[:, 0 : 2 * FIRST_PLANES, :].bitcast(I32), 0)
        nc.vector.memset(zeros[:], 0.0)
        nc.vector.memset(plane[:, 2 * FIRST_PLANES :, :].bitcast(I32), 0)
        nc.vector.memset(shifted[:].bitcast(I32), 0)

        xs_i = xs[:].bitcast(I32)
        xs_d = x_scales.bitcast(I32).rearrange("o f t -> (o f) t")
        nc.sync.dma_start(offs_t[:], offs)
        nc.scalar.dma_start(xs_i[0:112, :], xs_d[0:28, :].unsqueeze(0).broadcast_to([4, 28, T // 4]))
        nc.sync.dma_start(xs_i[112:128, :], xs_d[28:32, :].unsqueeze(0).broadcast_to([4, 4, T // 4]))
        nc.gpsimd.dma_start(xw[:].bitcast(I32), x_words.rearrange("o p t r -> p o (t r)").bitcast(I32))

        def load_w1_scales(a, b, queue):
            src = w1_scales[a:b].bitcast(I32).rearrange("e s q n -> q (e s) n")
            place = 2 * (a % PLANE_EXPERTS)
            for q in range(4):
                queue.dma_start(plane[32 * q : 32 * q + 4, place : place + 2 * (b - a), :].bitcast(I32), src[4 * q : 4 * q + 4, :, :])

        w1w = {}

        def load_w1_words(a, b):
            words = keep.tile([P, 2 * (b - a), 2 * H], U8, name="w1w%d" % a, align_bytes=64)
            nc.gpsimd.dma_start(words[:].bitcast(I32), w1_words[a:b].bitcast(I32).rearrange("e s p n -> p (e s) n"))
            for e in range(a, b):
                w1w[e] = words[:, 2 * (e - a) : 2 * (e - a) + 2, :]

        w2s = plane[:, 8:12, :].rearrange("p a n -> p (a n)")

        def load_w2_scales():
            src = w2_scales.bitcast(I32).rearrange("e s q n -> q (e s) n")
            for q in range(4):
                dst = w2s[32 * q : 32 * q + 4, 0 : E * N].bitcast(I32).rearrange("p (e n) -> p e n", e=E)
                nc.sync.dma_start(dst, src[4 * q : 4 * q + 4, :, :])

        gate_planes = keep.tile([P, 2, T], F32, name="gate_planes")
        gate_rows = keep.tile([P, P], F32, name="gate_rows")
        gate_cols = keep.tile([P, P], F32, name="gate_cols")
        nc.vector.memset(gate_rows[:], 0.0)

        slot_scales = {}
        buffer_of = {}

        def gather_scales(a, b, buffer):
            width = (b - a) * C
            pass0 = gathered[:, buffer, 0:width]
            pass1 = shifted[:, buffer, 0:width]
            nc.vector.tensor_copy(pass0, xs[:].indirect(offs_t[:, a * C // 16 : b * C // 16]))
            nc.sync.dma_start(pass1[0:112, :].bitcast(I32), pass0[16:128, :].bitcast(I32))
            for j in range(0, width, P):
                slot_scales[a * C + j] = (pass0[:, j : j + P], pass1[:, j : j + P])
            for e in range(a, b):
                buffer_of[e] = buffer

        slot_words = {}

        def gather_words(e):
            for o in range(2):
                slot_words[(e, o)] = gring.tile([P, C], U32, name="gw%d" % o, align_bytes=64)
            step = P if e == E - 1 else C
            for j in range(0, C, step):
                for o in range(2):
                    first = e * C + j
                    nc.vector.tensor_copy(slot_words[(e, o)][:, j : j + step], xw[:, o, :].indirect(offs_t[:, first // 16 : (first + step) // 16]))

        h_rows = {}

        def layer1(e, half):
            acc = sum_bank(e, half)
            order = (1, 0) if e in (1, 2, 3) else (0, 1)
            for o in order:
                nc.tensor.matmul_mx(
                    out=acc[:],
                    lhsT=slot_words[(e, o)][:, half * P : (half + 1) * P].bitcast(FP8X4),
                    lhsT_scale=slot_scales[e * C + half * P][o],
                    rhs=w1w[e][:, o, :].bitcast(FP4X4),
                    rhs_scale=plane[:, 2 * (e % PLANE_EXPERTS) + o, :],
                    start=(o == order[0]),
                    stop=(o == order[1]),
                )
            hr = hring.tile([P, H], BF16, name="hr")
            dst = hr[:].rearrange("j (u p d) -> j u p d", u=2, d=2)
            src = acc[:].rearrange("j (p u d) -> j u p d", u=2, d=2)
            nc.scalar.activation(dst, src, RELU)
            h_rows[(e, half)] = hr

        h_cols = keep.tile([P, 4 * S], BF16, name="h_cols", align_bytes=64)

        def turn(e, halves, bank, on_vector=False):
            count = len(halves)
            turned = bank[:, 0 : count * 2 * P].rearrange("p (a u j) -> p a u j", a=count, u=2)
            for a, half in enumerate(halves):
                pairs = h_rows[(e, half)][:].bitcast(F32)
                for u in range(2):
                    nc.tensor.transpose(turned[:, a, u, :], pairs[:, u * P : (u + 1) * P], ident[:])
            first = e * C + halves[0] * P
            dst = h_cols[:, 4 * first : 4 * (first + count * P)].bitcast(F32).rearrange("p (a j u) -> p a j u", a=count, u=2)
            src = turned.rearrange("p a u j -> p a j u")
            if on_vector:
                nc.vector.tensor_copy(dst, src)
            else:
                nc.scalar.copy(dst, src)

        load_w1_scales(0, FIRST_PLANES, nc.sync)
        load_w1_words(*WEIGHT_RUNS[0])
        nc.scalar.activation(ident[:], zeros[:], RELU)
        make_identity(nc, ident[:], nomemset=True)
        for e in range(SCALE_BUFFERS):
            gather_scales(e, e + 1, e)
        for e in range(AHEAD):
            gather_words(e)
        load_w1_scales(FIRST_PLANES, PLANE_EXPERTS, nc.gpsimd)
        for a, b in WEIGHT_RUNS[1:]:
            load_w1_words(a, b)
        nc.gpsimd.dma_start(w2w[:].bitcast(I32), w2_words.bitcast(I32).rearrange("e s p n -> p (e s) n"))
        nc.gpsimd.dma_start(gate_planes[:], gate[2:TOP].rearrange("r p t -> p r t"))
        nc.gpsimd.dma_start(gate_rows[0 : 2 * BLOCKS, :], gate[0:2, 0, :].rearrange("r (c m) -> r c m", m=P))

        def refill_scales(e):
            a = SCALE_BUFFERS + 2 * REFILL_AFTER.index(e)
            gather_scales(a, a + 2, buffer_of[e])

        for e in range(E):
            layer1(e, 0)
            layer1(e, 1)
            if e == E - 2:
                turn(e - 1, (0, 1), spare[0], on_vector=True)
            elif e == E - 1:
                turn(e - 1, (0, 1), spare[1], on_vector=True)
            elif e % 2 == 1:
                if e > 1:
                    turn(e - 2, (0, 1), sum_bank(e - 1, 0))
                turn(e - 1, (0, 1), sum_bank(e - 1, 1))
            if e == REFILL_AFTER[0]:
                refill_scales(e)
            if e + AHEAD < E:
                gather_words(e + AHEAD)
            if e in REFILL_AFTER[1:]:
                refill_scales(e)
            if e == E - PLANE_EXPERTS - 1:
                load_w1_scales(PLANE_EXPERTS, E, nc.sync)
                for r, pos in enumerate((pos1, pos2, pos3, pos4)):
                    nc.sync.dma_start(pos_t[r][:], pos)
            if e == 5:
                load_w2_scales()
        gate_rest = keep.tile([P, T - SPLIT], F32, name="w1w0", align_bytes=64)
        nc.sync.dma_start(gate_rest[:], gate[1, :, SPLIT:T])
        last = E - 1
        turn(last, (0,), spare[2])
        turn(last, (1,), spare[3])

        h_scales = keep.tile([P, S], U8, name="h_scales", align_bytes=64)
        h_late = keep.tile([P, S - EARLY], U32, name="h_late", align_bytes=64)
        h_early = keep.tile([P, EARLY], U32, name="w1w5", align_bytes=64)

        def h_words(a, b):
            return h_early[:, a:b] if a < EARLY else h_late[:, a - EARLY : b - EARLY]

        def layer2(a, b, bank):
            step = min(C, b - a)
            for j in range(a, b, step):
                e = j // C
                nc.tensor.matmul_mx(
                    out=bank[:, j - a : j - a + step],
                    lhsT=w2w[:, e, :].bitcast(FP4X4),
                    lhsT_scale=w2s[:, e * N : (e + 1) * N],
                    rhs=h_words(j, j + step).bitcast(FP8X4),
                    rhs_scale=h_scales[:, j : j + step],
                    start=True,
                    stop=True,
                )

        pieces = [
            (0, 2 * C, sum_bank(10, 0), False),
            (2 * C, 4 * C, sum_bank(10, 1), False),
            (4 * C, 6 * C, sum_bank(11, 0), False),
            (6 * C, 8 * C, sum_bank(11, 1), False),
            (8 * C, 10 * C, spare[0], True),
            (10 * C, last * C, spare[1], True),
            (last * C, last * C + P, spare[2], True),
            (last * C + P, S, spare[3], True),
        ]
        for a, b, bank, on_vector in pieces:
            nc.vector.quantize_mx(out=h_words(a, b).bitcast(FP8X4), scales=h_scales[:, a:b], in_=h_cols[:, 4 * a : 4 * b])
        for a, b, bank, on_vector in pieces:
            layer2(a, b, bank)
            if on_vector:
                nc.vector.tensor_copy(y_all[:, a:b], bank[:, 0 : b - a])
            else:
                nc.scalar.copy(y_all[:, a:b], bank[:, 0 : b - a])

        nc.tensor.transpose(sum_bank(10, 0)[:, 0:P], gate_rows[:], ident[:])
        nc.scalar.copy(gate_cols[:, 0 : 2 * BLOCKS], sum_bank(10, 0)[:, 0 : 2 * BLOCKS])

        picked = keep.tile([P, 2, T], F32, name="picked")
        scaled = keep.tile([P, 2, T], F32, name="scaled")
        prod = keep.tile([P, 2, T], F32, name="prod")
        prod_rest = keep.tile([P, T - SPLIT], F32, name="prod_rest")
        part_rest = keep.tile([P, T - SPLIT], F32, name="part_rest")
        pair = keep.tile([P, T], F32, name="pair")
        total = keep.tile([P, T], F32, name="total")

        def pick(r, a, b, bank):
            nc.scalar.activation(picked[:, r, a:b], y_all[:].indirect(pos_t[r][:, a // 16 : b // 16]), COPY)
            for j in range(a, b, P):
                nc.tensor.transpose(bank[:, j - a : j - a + P], picked[:, r, j : j + P], ident[:])

        def weigh(r, a, b, bank):
            for j in range(a, b, P):
                column = r * BLOCKS + j // P
                nc.scalar.activation(scaled[:, r, j : j + P], bank[:, j - a : j - a + P], COPY, scale=gate_cols[:, column : column + 1])

        def add_back(j, place, choices):
            for r in range(choices):
                nc.tensor.matmul(place, lhsT=scaled[:, r, j : j + P], rhs=ident[:], is_transpose=True, start=(r == 0), stop=(r == choices - 1))

        def fused(dst, r, a, b, weights):
            nc.vector.tensor_tensor(dst, y_all[:].indirect(pos_t[r][:, a // 16 : b // 16]), weights, MULT)

        first = 3 * P
        last_block = SPLIT - P
        pick(0, 0, first, sum_bank(10, 1))
        pick(1, 0, first, sum_bank(11, 0))
        pick(0, first, T, sum_bank(11, 1))
        pick(1, first, SPLIT, sum_bank(10, 0))
        weigh(0, 0, first, sum_bank(10, 1))
        weigh(1, 0, first, sum_bank(11, 0))
        for j in range(0, first, P):
            add_back(j, spare[1][:, j : j + P], 2)
        weigh(0, first, T, sum_bank(11, 1))
        add_back(SPLIT, spare[0][:, 0:P], 1)
        weigh(1, first, SPLIT, sum_bank(10, 0))
        add_back(first, spare[3][:, 0:P], 2)
        add_back(last_block, spare[2][:, 0:P], 2)

        fused(prod_rest[:], 1, SPLIT, T, gate_rest[:])
        fused(prod[:, 0, :], 2, 0, T, gate_planes[:, 0, :])
        fused(prod[:, 1, :], 3, 0, T, gate_planes[:, 1, :])
        nc.vector.tensor_tensor(part_rest[:], prod_rest[:], prod[:, 0, SPLIT:T], ADD)
        nc.vector.tensor_tensor(pair[:, 0:SPLIT], prod[:, 0, 0:SPLIT], prod[:, 1, 0:SPLIT], ADD)
        nc.vector.tensor_tensor(pair[:, SPLIT:T], part_rest[:], prod[:, 1, SPLIT:T], ADD)
        nc.vector.tensor_tensor(total[:, 0:first], pair[:, 0:first], spare[1][:, 0:first], ADD)
        nc.sync.dma_start(out[:, 0:first], total[:, 0:first])
        nc.vector.tensor_tensor(total[:, SPLIT:T], pair[:, SPLIT:T], spare[0][:, 0 : T - SPLIT], ADD)
        nc.sync.dma_start(out[:, SPLIT:T], total[:, SPLIT:T])
        nc.vector.tensor_tensor(total[:, first:last_block], pair[:, first:last_block], spare[3][:, 0:P], ADD)
        nc.vector.tensor_tensor(total[:, last_block:SPLIT], pair[:, last_block:SPLIT], spare[2][:, 0:P], ADD)
        nc.sync.dma_start(out[:, first:SPLIT], total[:, first:SPLIT])
